import numpy as np
import ml_dtypes


def mxq(x, axis, fmt="e4m3"):
    dtype, down = {"e4m3": (ml_dtypes.float8_e4m3fn, 7), "e5m2": (ml_dtypes.float8_e5m2, 14)}[fmt]
    v = np.moveaxis(np.asarray(x, np.float32).astype(ml_dtypes.bfloat16).astype(np.float64), axis, -1)
    blocks = v.reshape(v.shape[:-1] + (-1, 32))
    amax = np.abs(blocks).max(-1, keepdims=True)
    byte = np.maximum(np.where(amax > 0, np.frexp(amax)[1] - 1 + 127, 0) - down, 1)
    scale = np.exp2(byte - 127.0)
    codes = (blocks / scale).astype(np.float32).astype(dtype).astype(np.float64)
    return np.moveaxis((codes * scale).reshape(v.shape), -1, axis)


WIDE = False


def mx_kscale(k):
    if not WIDE:
        return np.ones(k)
    levels = np.array([10, -10, 5, -5, 0])
    if k % 512:
        return np.exp2(np.random.permutation(np.resize(levels, k // 32))).repeat(32)
    a = np.empty((k // 512, 16))
    for p in range(k // 512):
        a[p, :8] = np.random.permutation(np.resize(levels, 8))
        for g in range(8):
            far = levels[np.abs(levels - a[p, g]) >= 10]
            a[p, g + 8] = far[np.random.randint(len(far))]
    return np.exp2(a.ravel()).repeat(32)


def f64(x):
    return np.asarray(x).astype(np.float64)


def striped(idx):
    return np.tile(idx.reshape(-1, 16).T, (8, 1)).astype(np.uint16)


def unstriped(offs):
    return offs[:16].T.reshape(-1).astype(np.int64)


E2M1 = np.array([0.0, 0.5, 1.0, 1.5, 2.0, 3.0, 4.0, 6.0, -0.0, -0.5, -1.0, -1.5, -2.0, -3.0, -4.0, -6.0])


def pack_weight(w, fmt):
    k, n = w.shape
    w = f64(np.asarray(w, np.float32).astype(ml_dtypes.bfloat16)).reshape(k // 32, 32, n)
    amax = np.abs(w).max(1)
    if fmt == "e4m3":
        byte = np.frexp(amax)[1] - 1 + 127 - 7
    else:
        mant, ex = np.frexp(amax / 6.0)
        byte = np.where(mant > 0.5, ex, ex - 1) + 127
    byte = np.clip(np.where(amax > 0, byte, 1), 1, 254)
    scaled = (w * np.exp2(127.0 - byte)[:, None, :]).reshape(k, n).astype(np.float32)
    by_word = np.ascontiguousarray(scaled.reshape(k // 512, 128, 4, n).transpose(0, 1, 3, 2))
    if fmt == "e4m3":
        words = by_word.astype(ml_dtypes.float8_e4m3fn).view(np.uint8)
    else:
        c = by_word.astype(ml_dtypes.float4_e2m1fn).view(np.uint8) & 0xF
        words = (c[..., 0::2] | (c[..., 1::2] << 4)).reshape(k // 512, 128, 2 * n)
    return np.ascontiguousarray(words), np.ascontiguousarray(byte.astype(np.uint8).reshape(k // 512, 16, n))


def unpack_weight(words, scales, fmt):
    g, _, n = scales.shape
    words = np.ascontiguousarray(words).reshape(g, 128, n, -1)
    if fmt == "e4m3":
        vals = words.view(ml_dtypes.float8_e4m3fn).astype(np.float64)
    else:
        nib = np.empty((g, 128, n, 4), np.uint8)
        nib[..., 0::2] = words & 0xF
        nib[..., 1::2] = words >> 4
        vals = E2M1[nib]
    vals = vals * np.repeat(np.exp2(scales.astype(np.float64) - 127.0), 8, axis=1)[..., None]
    return vals.transpose(0, 1, 3, 2).reshape(g * 512, n)


def gelu(v):
    return 0.5 * v * (1.0 + np.tanh(np.sqrt(2.0 / np.pi) * (v + 0.044715 * v**3)))


K, T, S, T2, H, N = 512, 4096, 1024, 2048, 1024, 384

def setup_inputs():
    n = np.random.standard_normal
    s = mx_kscale(K)[:, None]
    u = mx_kscale(H)[:, None]
    tab_words, tab_scales = pack_weight(n((K, T)) * s, "e4m3")
    w2_words, w2_scales = pack_weight(n((K, H)) / np.sqrt(K) / s, "e2m1")
    return {
        "tab_words": tab_words, "tab_scales": tab_scales,
        "offs": striped(np.random.permutation(T)[:S]),
        "offs2": striped(np.random.permutation(T2)[:S]),
        "offs3": striped(np.random.permutation(T2)[:S]),
        "w1": (n((K, H)) / np.sqrt(K) / s).astype(np.float32),
        "w2_words": w2_words, "w2_scales": w2_scales,
        "w3": (n((H, N)) / np.sqrt(H) / u).astype(np.float32),
        "gain": (np.exp(0.3 * n(H)) * u[:, 0]).astype(np.float32),
        "bg": (n((H, T2)) * u).astype(np.float32),
        "wg1": np.exp(0.3 * n((128, S))).astype(np.float32),
        "wg2": np.exp(0.3 * n((128, S))).astype(np.float32),
    }

def reference(tab_words, tab_scales, offs, offs2, offs3, w1, w2_words, w2_scales, w3, gain, bg, wg1, wg2):
    v = unpack_weight(tab_words, tab_scales, "e4m3")[:, unstriped(offs)]
    W1 = mxq(f64(w1), 0, "e4m3")
    W2 = unpack_weight(w2_words, w2_scales, "e2m1")
    h1 = W1.T @ v
    h2 = (W2.T @ v) + np.tanh(h1)
    pageA = np.zeros((H, T2))
    pageA[:, unstriped(offs2)] = np.tile(f64(wg1), (H // 128, 1)) * h1
    pageB = np.zeros((H, T2))
    pageB[:, unstriped(offs3)] = np.tile(f64(wg2), (H // 128, 1)) * h2
    sig = 1 / (1 + np.exp(-pageB))
    z = f64(gain)[:, None] * pageA * sig + f64(bg)
    W3 = mxq(f64(w3), 0, "e4m3")
    return W3.T @ mxq(z, 0, "e4m3")

@@ -1,0 +1,286 @@
+from contextlib import ExitStack
+
+import concourse.mybir as mybir
+from concourse.masks import make_identity
+
+K, T, S, T2, H, N = 512, 4096, 1024, 2048, 1024, 384
+FLOPS = 2 * K * H * S * 2 + 2 * H * N * T2
+
+F32 = mybir.dt.float32
+BF16 = mybir.dt.bfloat16
+I32 = mybir.dt.int32
+U32 = mybir.dt.uint32
+U16 = mybir.dt.uint16
+U8 = mybir.dt.uint8
+FP8X4 = mybir.dt.float8_e4m3fn_x4
+FP4X4 = mybir.dt.float4_e2m1fn_x4
+MULT = mybir.AluOpType.mult
+ADD = mybir.AluOpType.add
+ACT = mybir.ActivationFunctionType
+
+P = 128
+PACK = 4
+BANK = 512
+TILES = H // P
+TILES_PER_PASS = 4
+PASSES = TILES // TILES_PER_PASS
+CHUNKS = T2 // BANK
+HALVES = S // BANK
+BLOCKS = BANK // P
+N_TILES = N // P
+W1_EARLY = 2
+
+
+def tile_list_peatland_ledger_features_kernel(
+    tc, tab_words, tab_scales, offs, offs2, offs3, w1, w2_words, w2_scales, w3, gain, bg, wg1, wg2, out
+):
+    nc = tc.nc
+    with ExitStack() as ctx:
+        keep = ctx.enter_context(tc.tile_pool(name="keep", bufs=1))
+        ring = ctx.enter_context(tc.tile_pool(name="ring", bufs=2))
+        psum = ctx.enter_context(tc.psum_pool(name="psum", bufs=1))
+
+        def bank(b, shape, name):
+            return psum.tile(shape, F32, name=name, tag="bank%d" % b)
+
+        def load_scale_rows(queue, plane, rows):
+            for q in range(4):
+                queue.dma_start(
+                    out=plane[32 * q : 32 * q + 4, :].bitcast(I32), in_=rows[4 * q : 4 * q + 4, :].bitcast(I32)
+                )
+
+        def round_and_interleave(grouped, raw):
+            nc.scalar.copy(
+                out=grouped.rearrange("p (c i) t -> p c t i", i=4), in_=raw.rearrange("p t (c i) -> p c t i", i=4)
+            )
+
+        def quantize(codes, scales, grouped):
+            nc.vector.quantize_mx(out=codes.bitcast(FP8X4), scales=scales, in_=grouped)
+
+        ident = keep.tile([P, P], F32, name="ident")
+        nc.vector.memset(ident[:], 0.0)
+        tab_s = keep.tile([P, T], U8, name="tab_s", tag="tab_s", align_bytes=64)
+        nc.vector.memset(tab_s[:].bitcast(I32), 0)
+        gain_rows = keep.tile([P, P], F32, name="gain_rows", tag="late")
+        nc.gpsimd.memset(gain_rows[:], 0.0)
+        make_identity(nc, ident[:], nomemset=True)
+
+        list_tab = keep.tile([P, S // 16], U16, name="list_tab")
+        nc.sync.dma_start(list_tab[:], offs)
+        nc.sync.dma_start(out=gain_rows[0:TILES, :], in_=gain.rearrange("(c p) -> c p", p=P))
+        w1_rows = w1.rearrange("(p t) r -> p t r", t=PACK)
+        w1_first = keep.tile([P, PACK, P], F32, name="w1_first")
+        nc.sync.dma_start(out=w1_first[:], in_=w1_rows[:, :, 0:P])
+        load_scale_rows(nc.scalar, tab_s, tab_scales[0])
+        tab_w = keep.tile([P, T], I32, name="tab_w", tag="tab_w", align_bytes=64)
+        nc.sync.dma_start(out=tab_w[:], in_=tab_words[0].rearrange("p t i -> p (t i)").bitcast(I32))
+        list_a = keep.tile([P, S // 16], U16, name="list_a")
+        nc.sync.dma_start(list_a[:], offs2)
+        list_b = keep.tile([P, S // 16], U16, name="list_b")
+        nc.sync.dma_start(list_b[:], offs3)
+
+        pages_a = [keep.tile([P, T2], F32, name="page_a%d" % i) for i in range(2)]
+        pages_b = [keep.tile([P, T2], F32, name="page_b%d" % i) for i in range(2)]
+        nc.vector.memset(pages_a[0][:], 0.0)
+        nc.vector.memset(pages_b[0][:], 0.0)
+        nc.gpsimd.memset(pages_b[1][:], 0.0)
+        nc.gpsimd.memset(pages_a[1][:], 0.0)
+
+        gain_t = bank(7, [P, P], "gain_t")
+        nc.tensor.transpose(gain_t[:], gain_rows[:], ident[:])
+        gain_col = keep.tile([P, TILES], F32, name="gain_col")
+        nc.scalar.activation(out=gain_col[:], in_=gain_t[:, 0:TILES], func=ACT.Copy)
+
+        late = H - W1_EARLY * P
+        late_loads = keep.tile([P, 2 * S + PACK * P], F32, name="late_loads", tag="late")
+        wg_a, wg_b = late_loads[:, 0:S], late_loads[:, S : 2 * S]
+        w1_second = late_loads[:, 2 * S : 2 * S + PACK * P].rearrange("p (t r) -> p t r", t=PACK)
+        nc.sync.dma_start(out=w1_second, in_=w1_rows[:, :, P : 2 * P])
+        nc.sync.dma_start(out=wg_a, in_=wg1)
+
+        v_scales = keep.tile([P, S], U8, name="v_scales", align_bytes=64)
+        nc.vector.tensor_copy(v_scales[:], tab_s[:].indirect(list_tab[:]))
+        w_codes = keep.tile([P, H + PASSES * N], U32, name="w_codes", align_bytes=64)
+        w_scales = keep.tile([P, H + PASSES * N], U8, name="w_scales", align_bytes=64)
+
+        def quantize_w1_early(c):
+            grouped = keep.tile([P, P, PACK], BF16, name="w1_grouped%d" % c, tag=("w2_w", "bg_even")[c], align_bytes=64)
+            round_and_interleave(grouped[:], (w1_first[:], w1_second)[c])
+            cols = slice(c * P, (c + 1) * P)
+            quantize(w_codes[:, cols], w_scales[:, cols], grouped[:].rearrange("p c t -> p (c t)"))
+
+        quantize_w1_early(0)
+        w2_w = keep.tile([P, 2 * H], U8, name="w2_w", tag="w2_w", align_bytes=64)
+        nc.sync.dma_start(out=w2_w[:].bitcast(I32), in_=w2_words[0].bitcast(I32))
+        w2_s = keep.tile([P, H], U8, name="w2_s", tag="tab_s", align_bytes=64)
+        nc.vector.memset(w2_s[:].bitcast(I32), 0)
+        load_scale_rows(nc.sync, w2_s, w2_scales[0])
+        nc.sync.dma_start(out=wg_b, in_=wg2)
+        v_words = []
+        for h in range(HALVES):
+            words = keep.tile([P, BANK], U32, name="v_words%d" % h, align_bytes=64)
+            per = BANK // 16
+            nc.vector.tensor_copy(words[:], tab_w[:].bitcast(U32).indirect(list_tab[:, h * per : (h + 1) * per]))
+            v_words.append(words)
+        quantize_w1_early(1)
+
+        w_late = keep.tile([P, PACK * (late + PASSES * N)], F32, name="w_late", tag="tab_w", align_bytes=64)
+        w1_late = w_late[:, 0 : PACK * late].rearrange("p (t r) -> p t r", t=PACK)
+        nc.sync.dma_start(out=w1_late, in_=w1_rows[:, :, W1_EARLY * P : H])
+        w3_raw = []
+        for a in range(PASSES):
+            w0 = PACK * (late + a * N)
+            w3_raw.append(w_late[:, w0 : w0 + PACK * N].rearrange("p (t n) -> p t n", t=PACK))
+            nc.sync.dma_start(out=w3_raw[a], in_=w3[a * 512 : (a + 1) * 512, :].rearrange("(p t) n -> p t n", t=PACK))
+
+        def quantize_late_weights():
+            first = W1_EARLY * P
+            grouped = keep.tile([P, late + PASSES * N, PACK], BF16, name="w_grouped", tag="grouped1", align_bytes=64)
+            for c0 in range(0, late, 256):
+                round_and_interleave(grouped[:, c0 : c0 + 256, :], w1_late[:, :, c0 : c0 + 256])
+            for a in range(PASSES):
+                round_and_interleave(grouped[:, late + a * N : late + (a + 1) * N, :], w3_raw[a])
+            flat = grouped[:].rearrange("p c t -> p (c t)")
+            for c0, c1 in ((0, 1024), (1024, late + PASSES * N)):
+                quantize(w_codes[:, first + c0 : first + c1], w_scales[:, first + c0 : first + c1], flat[:, PACK * c0 : PACK * c1])
+
+        gained, src_b, tanh_h1, bg_rows = {}, {}, {}, {}
+
+        def load_bg(c):
+            bg_rows[c] = keep.tile([P, T2], F32, name="bg_rows", tag=("bg_even", "tab_w")[c % 2], align_bytes=64)
+            nc.sync.dma_start(out=bg_rows[c][:], in_=bg[c * P : (c + 1) * P, :])
+
+        def first_products(c):
+            gained[c] = keep.tile([P, S], F32, name="gained", tag="slot%d" % (c % 3))
+            src_b[c] = ring.tile([P, S], F32, name="src_b", bufs=3)
+            tanh_h1[c] = ring.tile([P, S], F32, name="tanh_h1", bufs=3)
+            rows = slice(c * P, (c + 1) * P)
+            for h in range(HALVES):
+                cols = slice(h * BANK, (h + 1) * BANK)
+                h1 = bank(4 + h, [P, BANK], "h1")
+                nc.tensor.matmul_mx(
+                    out=h1[:], lhsT=w_codes[:, rows].bitcast(FP8X4), lhsT_scale=w_scales[:, rows],
+                    rhs=v_words[h][:].bitcast(FP8X4), rhs_scale=v_scales[:, cols], start=True, stop=True,
+                )
+                nc.scalar.activation(out=gained[c][:, cols], in_=h1[:], func=ACT.Copy, scale=gain_col[:, c : c + 1])
+                nc.scalar.activation(out=tanh_h1[c][:, cols], in_=h1[:], func=ACT.Tanh)
+            for h in range(HALVES):
+                cols = slice(h * BANK, (h + 1) * BANK)
+                h2 = bank(h, [P, BANK], "h2")
+                nc.tensor.matmul_mx(
+                    out=h2[:], lhsT=w2_w[:, 2 * c * P : 2 * (c + 1) * P].bitcast(FP4X4), lhsT_scale=w2_s[:, rows],
+                    rhs=v_words[h][:].bitcast(FP8X4), rhs_scale=v_scales[:, cols], start=True, stop=True,
+                )
+                nc.scalar.copy(out=src_b[c][:, cols], in_=h2[:])
+
+        def weigh(c):
+            nc.gpsimd.tensor_tensor(src_b[c][:], src_b[c][:], tanh_h1[c][:], ADD)
+            nc.gpsimd.tensor_tensor(src_b[c][:], src_b[c][:], wg_b, MULT)
+            if c > 0:
+                nc.gpsimd.tensor_tensor(tanh_h1[c][:], gained[c][:], wg_a, MULT)
+
+        gate = {}
+
+        def scatter(c):
+            page_a, page_b = pages_a[c % 2], pages_b[c % 2]
+            if c == 0:
+                per = BANK // 16
+                for h in range(HALVES):
+                    cols = slice(h * BANK, (h + 1) * BANK)
+                    nc.vector.tensor_tensor(
+                        page_a[:].indirect(list_a[:, h * per : (h + 1) * per]), gained[c][:, cols], wg_a[:, cols], MULT
+                    )
+            nc.vector.tensor_copy(page_b[:].indirect(list_b[:]), src_b[c][:])
+            gate[c] = keep.tile([P, T2], F32, name="gate", tag="slot%d" % (c % 3))
+            nc.scalar.activation(out=gate[c][:], in_=page_b[:], func=ACT.Sigmoid)
+            if c > 0:
+                nc.vector.tensor_copy(page_a[:].indirect(list_a[:]), tanh_h1[c][:])
+
+        z_t = {}
+
+        def combine(c):
+            a, quarter = divmod(c, TILES_PER_PASS)
+            last = c == TILES - 1
+            width = BANK if last else 2 * BANK
+            engine = nc.vector if last else nc.gpsimd
+            gated = keep.tile([P, T2], F32, name="gated", tag="slot%d" % ((c + 1) % 3))
+            for c0 in range(0, T2, width):
+                cols = slice(c0, c0 + width)
+                engine.tensor_tensor(gated[:, cols], pages_a[c % 2][:, cols], gate[c][:, cols], MULT)
+            for q in range(CHUNKS):
+                if quarter == 0:
+                    z_t[a, q] = keep.tile([P, BLOCKS, 2, P, 2], BF16, name="z_t%d" % q, tag="z_t%d" % q)
+                zt = bank(2 + q, [P, BLOCKS, P], "zt")
+                for i, src in enumerate((bg_rows[c], gated)):
+                    for b in range(BLOCKS):
+                        m0 = q * BANK + b * P
+                        nc.tensor.matmul(
+                            zt[:, b, :], lhsT=src[:, m0 : m0 + P], rhs=ident[:], is_transpose=True,
+                            start=(i == 0 and b == 0), stop=(i == 1 and b == BLOCKS - 1),
+                        )
+                nc.scalar.copy(
+                    out=z_t[a, q][:, :, :, 32 * quarter : 32 * (quarter + 1), :],
+                    in_=zt[:].rearrange("m b (p u e) -> m b u p e", u=2, e=2),
+                )
+
+        z_codes = [keep.tile([P, T2], U32, name="z_codes%d" % a, align_bytes=64) for a in range(PASSES)]
+        z_scales = [keep.tile([P, T2], U8, name="z_scales%d" % a, align_bytes=64) for a in range(PASSES)]
+
+        def turn_back(a, q, grouped_words, engines):
+            words = z_t[a, q][:].rearrange("m b u p e -> m (b u p e)").bitcast(F32)
+            for pair in range(2):
+                xt = bank(6 + pair, [P, 2, 2, P], "xt")
+                for b in range(2):
+                    for u in range(2):
+                        w0 = ((2 * pair + b) * 2 + u) * P
+                        nc.tensor.transpose(xt[:, b, u, :], words[:, w0 : w0 + P], ident[:])
+                dst = grouped_words[:, pair * BANK : (pair + 1) * BANK].rearrange("p (b m u) -> p b m u", b=2, u=2)
+                engines[pair](out=dst, in_=xt[:].rearrange("p b u m -> p b m u"))
+
+        def quantize_z(a, chunks, tag, engines):
+            grouped = keep.tile([P, len(chunks) * BANK * PACK], BF16, name="z_grouped", tag=tag, align_bytes=64)
+            for i, q in enumerate(chunks):
+                turn_back(a, q, grouped[:, i * BANK * PACK : (i + 1) * BANK * PACK].bitcast(F32), engines)
+            cols = slice(chunks[0] * BANK, (chunks[-1] + 1) * BANK)
+            quantize(z_codes[a][:, cols], z_scales[a][:, cols], grouped[:])
+
+        def last_product(q):
+            cols = slice(q * BANK, (q + 1) * BANK)
+            for nt in range(N_TILES):
+                acc = bank((q * N_TILES + nt) % 6, [P, BANK], "acc")
+                for a in range(PASSES):
+                    w0 = H + a * N + nt * P
+                    nc.tensor.matmul_mx(
+                        out=acc[:], lhsT=w_codes[:, w0 : w0 + P].bitcast(FP8X4), lhsT_scale=w_scales[:, w0 : w0 + P],
+                        rhs=z_codes[a][:, cols].bitcast(FP8X4), rhs_scale=z_scales[a][:, cols],
+                        start=(a == 0), stop=(a == PASSES - 1),
+                    )
+                result = ring.tile([P, BANK], F32, name="result", bufs=6)
+                if nt == 1:
+                    nc.vector.tensor_copy(out=result[:], in_=acc[:])
+                else:
+                    nc.scalar.copy(out=result[:], in_=acc[:])
+                nc.sync.dma_start(out=out[nt * P : (nt + 1) * P, cols], in_=result[:])
+
+        first_products(0)
+        weigh(0)
+        load_bg(0)
+        first_products(1)
+        weigh(1)
+        quantize_late_weights()
+        first_products(2)
+        for c in range(TILES):
+            if c + 1 < TILES:
+                load_bg(c + 1)
+            scatter(c)
+            combine(c)
+            if c == TILES_PER_PASS - 1:
+                for half in range(2):
+                    quantize_z(0, [2 * half, 2 * half + 1], "grouped%d" % half, (nc.scalar.copy, nc.scalar.copy))
+            if c + 2 < TILES:
+                weigh(c + 2)
+            if c + 3 < TILES:
+                first_products(c + 3)
+        for q in range(CHUNKS):
+            quantize_z(1, [q], "grouped%d" % (q % 2), (nc.scalar.copy, nc.vector.tensor_copy))
+            last_product(q)

@@ -1,7 +1,6 @@
 from contextlib import ExitStack
 
 import concourse.mybir as mybir
-from concourse.masks import make_identity
 
 K, T, S, T2, H, N = 512, 4096, 1024, 2048, 1024, 384
 FLOPS = 2 * K * H * S * 2 + 2 * H * N * T2
@@ -57,62 +56,66 @@ def tile_list_peatland_ledger_features_kernel(
         def quantize(codes, scales, grouped):
             nc.vector.quantize_mx(out=codes.bitcast(FP8X4), scales=scales, in_=grouped)
 
-        ident = keep.tile([P, P], F32, name="ident")
-        nc.vector.memset(ident[:], 0.0)
         tab_s = keep.tile([P, T], U8, name="tab_s", tag="tab_s", align_bytes=64)
         nc.vector.memset(tab_s[:].bitcast(I32), 0)
-        gain_rows = keep.tile([P, P], F32, name="gain_rows", tag="late")
-        nc.gpsimd.memset(gain_rows[:], 0.0)
-        make_identity(nc, ident[:], nomemset=True)
+        zeros = keep.tile([P, P], F32, name="zeros", tag="tab_w", align_bytes=64)
+        nc.vector.memset(zeros[:], 0.0)
+        ident = keep.tile([P, P], F32, name="ident")
+        nc.gpsimd.affine_select(
+            out=ident[:], in_=zeros[:], compare_op=mybir.AluOpType.not_equal, fill=1.0, base=0,
+            pattern=[[-1, P]], channel_multiplier=1,
+        )
 
         list_tab = keep.tile([P, S // 16], U16, name="list_tab")
         nc.sync.dma_start(list_tab[:], offs)
-        nc.sync.dma_start(out=gain_rows[0:TILES, :], in_=gain.rearrange("(c p) -> c p", p=P))
-        w1_rows = w1.rearrange("(p t) r -> p t r", t=PACK)
-        w1_first = keep.tile([P, PACK, P], F32, name="w1_first")
-        nc.sync.dma_start(out=w1_first[:], in_=w1_rows[:, :, 0:P])
-        load_scale_rows(nc.scalar, tab_s, tab_scales[0])
-        tab_w = keep.tile([P, T], I32, name="tab_w", tag="tab_w", align_bytes=64)
-        nc.sync.dma_start(out=tab_w[:], in_=tab_words[0].rearrange("p t i -> p (t i)").bitcast(I32))
         list_a = keep.tile([P, S // 16], U16, name="list_a")
         nc.sync.dma_start(list_a[:], offs2)
         list_b = keep.tile([P, S // 16], U16, name="list_b")
         nc.sync.dma_start(list_b[:], offs3)
+        w1_rows = w1.rearrange("(p t) r -> p t r", t=PACK)
+        w1_first = keep.tile([P, PACK, P], F32, name="w1_first", tag="late")
+        nc.sync.dma_start(out=w1_first[:], in_=w1_rows[:, :, 0:P])
+        load_scale_rows(nc.sync, tab_s, tab_scales[0])
+        tab_w = keep.tile([P, T], I32, name="tab_w", tag="tab_w", align_bytes=64)
+        nc.sync.dma_start(out=tab_w[:], in_=tab_words[0].rearrange("p t i -> p (t i)").bitcast(I32))
+        gain_rows = keep.tile([P, P], F32, name="gain_rows")
+        nc.vector.memset(gain_rows[:], 0.0)
+        nc.sync.dma_start(out=gain_rows[0:TILES, :], in_=gain.rearrange("(c p) -> c p", p=P))
 
-        pages_a = [keep.tile([P, T2], F32, name="page_a%d" % i) for i in range(2)]
+        pages_a = [keep.tile([P, T2], F32, name="page_a0")]
         pages_b = [keep.tile([P, T2], F32, name="page_b%d" % i) for i in range(2)]
         nc.vector.memset(pages_a[0][:], 0.0)
         nc.vector.memset(pages_b[0][:], 0.0)
-        nc.gpsimd.memset(pages_b[1][:], 0.0)
-        nc.gpsimd.memset(pages_a[1][:], 0.0)
+        nc.vector.memset(pages_b[1][:], 0.0)
 
         gain_t = bank(7, [P, P], "gain_t")
         nc.tensor.transpose(gain_t[:], gain_rows[:], ident[:])
         gain_col = keep.tile([P, TILES], F32, name="gain_col")
         nc.scalar.activation(out=gain_col[:], in_=gain_t[:, 0:TILES], func=ACT.Copy)
 
+        v_scales = keep.tile([P, S], U8, name="v_scales", align_bytes=64)
+        nc.vector.tensor_copy(v_scales[:], tab_s[:].indirect(list_tab[:]))
+        pages_a.append(keep.tile([P, T2], F32, name="page_a1", tag="tab_s", align_bytes=64))
+        nc.gpsimd.memset(pages_a[1][:], 0.0)
+        w_codes = keep.tile([P, H + PASSES * N], U32, name="w_codes", align_bytes=64)
+        w_scales = keep.tile([P, H + PASSES * N], U8, name="w_scales", align_bytes=64)
+
+        def quantize_w1_early(c, raw):
+            grouped = keep.tile([P, P, PACK], BF16, name="w1_grouped%d" % c, tag=("w2_w", "bg_even")[c], align_bytes=64)
+            round_and_interleave(grouped[:], raw)
+            cols = slice(c * P, (c + 1) * P)
+            quantize(w_codes[:, cols], w_scales[:, cols], grouped[:].rearrange("p c t -> p (c t)"))
+
+        quantize_w1_early(0, w1_first[:])
         late = H - W1_EARLY * P
         late_loads = keep.tile([P, 2 * S + PACK * P], F32, name="late_loads", tag="late")
         wg_a, wg_b = late_loads[:, 0:S], late_loads[:, S : 2 * S]
         w1_second = late_loads[:, 2 * S : 2 * S + PACK * P].rearrange("p (t r) -> p t r", t=PACK)
         nc.sync.dma_start(out=w1_second, in_=w1_rows[:, :, P : 2 * P])
         nc.sync.dma_start(out=wg_a, in_=wg1)
-
-        v_scales = keep.tile([P, S], U8, name="v_scales", align_bytes=64)
-        nc.vector.tensor_copy(v_scales[:], tab_s[:].indirect(list_tab[:]))
-        w_codes = keep.tile([P, H + PASSES * N], U32, name="w_codes", align_bytes=64)
-        w_scales = keep.tile([P, H + PASSES * N], U8, name="w_scales", align_bytes=64)
-
-        def quantize_w1_early(c):
-            grouped = keep.tile([P, P, PACK], BF16, name="w1_grouped%d" % c, tag=("w2_w", "bg_even")[c], align_bytes=64)
-            round_and_interleave(grouped[:], (w1_first[:], w1_second)[c])
-            cols = slice(c * P, (c + 1) * P)
-            quantize(w_codes[:, cols], w_scales[:, cols], grouped[:].rearrange("p c t -> p (c t)"))
-
-        quantize_w1_early(0)
         w2_w = keep.tile([P, 2 * H], U8, name="w2_w", tag="w2_w", align_bytes=64)
         nc.sync.dma_start(out=w2_w[:].bitcast(I32), in_=w2_words[0].bitcast(I32))
-        w2_s = keep.tile([P, H], U8, name="w2_s", tag="tab_s", align_bytes=64)
+        w2_s = keep.tile([P, H], U8, name="w2_s", align_bytes=64)
         nc.vector.memset(w2_s[:].bitcast(I32), 0)
         load_scale_rows(nc.sync, w2_s, w2_scales[0])
         nc.sync.dma_start(out=wg_b, in_=wg2)
@@ -122,27 +125,26 @@ def tile_list_peatland_ledger_features_kernel(
             per = BANK // 16
             nc.vector.tensor_copy(words[:], tab_w[:].bitcast(U32).indirect(list_tab[:, h * per : (h + 1) * per]))
             v_words.append(words)
-        quantize_w1_early(1)
+        quantize_w1_early(1, w1_second)
 
         w_late = keep.tile([P, PACK * (late + PASSES * N)], F32, name="w_late", tag="tab_w", align_bytes=64)
-        w1_late = w_late[:, 0 : PACK * late].rearrange("p (t r) -> p t r", t=PACK)
-        nc.sync.dma_start(out=w1_late, in_=w1_rows[:, :, W1_EARLY * P : H])
-        w3_raw = []
-        for a in range(PASSES):
-            w0 = PACK * (late + a * N)
-            w3_raw.append(w_late[:, w0 : w0 + PACK * N].rearrange("p (t n) -> p t n", t=PACK))
-            nc.sync.dma_start(out=w3_raw[a], in_=w3[a * 512 : (a + 1) * 512, :].rearrange("(p t) n -> p t n", t=PACK))
+        raw_parts = []
+        w0 = 0
+        for src in (w1_rows[:, :, 256:512], w1_rows[:, :, 512:H], w3[0:512, :].rearrange("(p t) n -> p t n", t=PACK), w3[512:H, :].rearrange("(p t) n -> p t n", t=PACK)):
+            width = src.shape[2]
+            raw_parts.append(w_late[:, PACK * w0 : PACK * (w0 + width)].rearrange("p (t r) -> p t r", t=PACK))
+            nc.sync.dma_start(out=raw_parts[-1], in_=src)
+            w0 = w0 + width
 
-        def quantize_late_weights():
-            first = W1_EARLY * P
-            grouped = keep.tile([P, late + PASSES * N, PACK], BF16, name="w_grouped", tag="grouped1", align_bytes=64)
-            for c0 in range(0, late, 256):
-                round_and_interleave(grouped[:, c0 : c0 + 256, :], w1_late[:, :, c0 : c0 + 256])
-            for a in range(PASSES):
-                round_and_interleave(grouped[:, late + a * N : late + (a + 1) * N, :], w3_raw[a])
-            flat = grouped[:].rearrange("p c t -> p (c t)")
-            for c0, c1 in ((0, 1024), (1024, late + PASSES * N)):
-                quantize(w_codes[:, first + c0 : first + c1], w_scales[:, first + c0 : first + c1], flat[:, PACK * c0 : PACK * c1])
+        def quantize_weights(first, parts, tag):
+            width = sum(part.shape[2] for part in parts)
+            grouped = keep.tile([P, width, PACK], BF16, name="w_grouped", tag=tag, align_bytes=64)
+            c0 = 0
+            for part in parts:
+                round_and_interleave(grouped[:, c0 : c0 + part.shape[2], :], part)
+                c0 = c0 + part.shape[2]
+            cols = slice(first, first + width)
+            quantize(w_codes[:, cols], w_scales[:, cols], grouped[:].rearrange("p c t -> p (c t)"))
 
         gained, src_b, tanh_h1, bg_rows = {}, {}, {}, {}
 
@@ -226,10 +228,10 @@ def tile_list_peatland_ledger_features_kernel(
         z_codes = [keep.tile([P, T2], U32, name="z_codes%d" % a, align_bytes=64) for a in range(PASSES)]
         z_scales = [keep.tile([P, T2], U8, name="z_scales%d" % a, align_bytes=64) for a in range(PASSES)]
 
-        def turn_back(a, q, grouped_words, engines):
+        def turn_back(a, q, grouped_words, engines, banks):
             words = z_t[a, q][:].rearrange("m b u p e -> m (b u p e)").bitcast(F32)
             for pair in range(2):
-                xt = bank(6 + pair, [P, 2, 2, P], "xt")
+                xt = bank(banks[pair], [P, 2, 2, P], "xt")
                 for b in range(2):
                     for u in range(2):
                         w0 = ((2 * pair + b) * 2 + u) * P
@@ -237,17 +239,17 @@ def tile_list_peatland_ledger_features_kernel(
                 dst = grouped_words[:, pair * BANK : (pair + 1) * BANK].rearrange("p (b m u) -> p b m u", b=2, u=2)
                 engines[pair](out=dst, in_=xt[:].rearrange("p b u m -> p b m u"))
 
-        def quantize_z(a, chunks, tag, engines):
+        def quantize_z(a, chunks, tag, engines, banks):
             grouped = keep.tile([P, len(chunks) * BANK * PACK], BF16, name="z_grouped", tag=tag, align_bytes=64)
             for i, q in enumerate(chunks):
-                turn_back(a, q, grouped[:, i * BANK * PACK : (i + 1) * BANK * PACK].bitcast(F32), engines)
+                turn_back(a, q, grouped[:, i * BANK * PACK : (i + 1) * BANK * PACK].bitcast(F32), engines, banks)
             cols = slice(chunks[0] * BANK, (chunks[-1] + 1) * BANK)
             quantize(z_codes[a][:, cols], z_scales[a][:, cols], grouped[:])
 
         def last_product(q):
             cols = slice(q * BANK, (q + 1) * BANK)
             for nt in range(N_TILES):
-                acc = bank((q * N_TILES + nt) % 6, [P, BANK], "acc")
+                acc = bank(2 + (q * N_TILES + nt) % 4, [P, BANK], "acc")
                 for a in range(PASSES):
                     w0 = H + a * N + nt * P
                     nc.tensor.matmul_mx(
@@ -267,20 +269,25 @@ def tile_list_peatland_ledger_features_kernel(
         load_bg(0)
         first_products(1)
         weigh(1)
-        quantize_late_weights()
+        quantize_weights(256, [raw_parts[0]], "grouped0")
         first_products(2)
         for c in range(TILES):
             if c + 1 < TILES:
                 load_bg(c + 1)
             scatter(c)
+            if c == 0:
+                quantize_weights(512, [raw_parts[1][:, :, 0:256], raw_parts[1][:, :, 256:512], raw_parts[2], raw_parts[3][:, :, 0:128]], "grouped1")
+                quantize_weights(1536, [raw_parts[3][:, :, 128:N]], "grouped0")
             combine(c)
             if c == TILES_PER_PASS - 1:
                 for half in range(2):
-                    quantize_z(0, [2 * half, 2 * half + 1], "grouped%d" % half, (nc.scalar.copy, nc.scalar.copy))
+                    quantize_z(0, [2 * half, 2 * half + 1], "grouped%d" % half, (nc.scalar.copy, nc.scalar.copy), (6, 7))
             if c + 2 < TILES:
                 weigh(c + 2)
             if c + 3 < TILES:
                 first_products(c + 3)
-        for q in range(CHUNKS):
-            quantize_z(1, [q], "grouped%d" % (q % 2), (nc.scalar.copy, nc.vector.tensor_copy))
-            last_product(q)
+        for q in range(CHUNKS + 1):
+            if q < CHUNKS:
+                quantize_z(1, [q], "grouped%d" % (q % 2), (nc.scalar.copy, nc.vector.tensor_copy), ((6, 7), (0, 1))[q % 2])
+            if q >= 1:
+                last_product(q - 1)

@@ -27,7 +27,6 @@ CHUNKS = T2 // BANK
 HALVES = S // BANK
 BLOCKS = BANK // P
 N_TILES = N // P
-W1_EARLY = 2
 
 
 def tile_list_peatland_ledger_features_kernel(
@@ -73,14 +72,18 @@ def tile_list_peatland_ledger_features_kernel(
         list_b = keep.tile([P, S // 16], U16, name="list_b")
         nc.sync.dma_start(list_b[:], offs3)
         w1_rows = w1.rearrange("(p t) r -> p t r", t=PACK)
-        w1_first = keep.tile([P, PACK, P], F32, name="w1_first", tag="late")
-        nc.sync.dma_start(out=w1_first[:], in_=w1_rows[:, :, 0:P])
+        w1_first = keep.tile([P, PACK, 256], F32, name="w1_first", tag="w2_w", align_bytes=64)
+        nc.sync.dma_start(out=w1_first[:], in_=w1_rows[:, :, 0:256])
         load_scale_rows(nc.sync, tab_s, tab_scales[0])
         tab_w = keep.tile([P, T], I32, name="tab_w", tag="tab_w", align_bytes=64)
         nc.sync.dma_start(out=tab_w[:], in_=tab_words[0].rearrange("p t i -> p (t i)").bitcast(I32))
-        gain_rows = keep.tile([P, P], F32, name="gain_rows")
+        gain_rows = keep.tile([P, P], F32, name="gain_rows", tag="bg_even", align_bytes=64)
         nc.vector.memset(gain_rows[:], 0.0)
         nc.sync.dma_start(out=gain_rows[0:TILES, :], in_=gain.rearrange("(c p) -> c p", p=P))
+
+        w2_s = keep.tile([P, H], U8, name="w2_s", align_bytes=64)
+        nc.vector.memset(w2_s[:].bitcast(I32), 0)
+        load_scale_rows(nc.sync, w2_s, w2_scales[0])
 
         pages_a = [keep.tile([P, T2], F32, name="page_a0")]
         pages_b = [keep.tile([P, T2], F32, name="page_b%d" % i) for i in range(2)]
@@ -93,31 +96,38 @@ def tile_list_peatland_ledger_features_kernel(
         gain_col = keep.tile([P, TILES], F32, name="gain_col")
         nc.scalar.activation(out=gain_col[:], in_=gain_t[:, 0:TILES], func=ACT.Copy)
 
+        w_scales = keep.tile([P, H + PASSES * N], U8, name="w_scales", align_bytes=64)
+        w_codes = {}
+
+        def group_weights(parts, grouped_tag):
+            width = sum(part.shape[2] for part in parts)
+            grouped = keep.tile([P, width, PACK], BF16, name="w_grouped", tag=grouped_tag, align_bytes=64)
+            c0 = 0
+            for part in parts:
+                round_and_interleave(grouped[:, c0 : c0 + part.shape[2], :], part)
+                c0 = c0 + part.shape[2]
+            return grouped
+
+        def quantize_weights(first, grouped, codes_tag):
+            width = grouped.shape[1]
+            codes = keep.tile([P, width], U32, name="w_codes", tag=codes_tag, align_bytes=64)
+            quantize(codes[:], w_scales[:, first : first + width], grouped[:].rearrange("p c t -> p (c t)"))
+            for c0 in range(0, width, P):
+                w_codes[first + c0] = codes[:, c0 : c0 + P].bitcast(FP8X4)
+
+        quantize_weights(0, group_weights([w1_first[:]], "page_a1"), "w_codes0")
+        pages_a.append(keep.tile([P, T2], F32, name="page_a1", tag="page_a1", align_bytes=64))
+        nc.gpsimd.memset(pages_a[1][:], 0.0)
         v_scales = keep.tile([P, S], U8, name="v_scales", align_bytes=64)
         nc.vector.tensor_copy(v_scales[:], tab_s[:].indirect(list_tab[:]))
-        pages_a.append(keep.tile([P, T2], F32, name="page_a1", tag="tab_s", align_bytes=64))
-        nc.gpsimd.memset(pages_a[1][:], 0.0)
-        w_codes = keep.tile([P, H + PASSES * N], U32, name="w_codes", align_bytes=64)
-        w_scales = keep.tile([P, H + PASSES * N], U8, name="w_scales", align_bytes=64)
-
-        def quantize_w1_early(c, raw):
-            grouped = keep.tile([P, P, PACK], BF16, name="w1_grouped%d" % c, tag=("w2_w", "bg_even")[c], align_bytes=64)
-            round_and_interleave(grouped[:], raw)
-            cols = slice(c * P, (c + 1) * P)
-            quantize(w_codes[:, cols], w_scales[:, cols], grouped[:].rearrange("p c t -> p (c t)"))
-
-        quantize_w1_early(0, w1_first[:])
-        late = H - W1_EARLY * P
-        late_loads = keep.tile([P, 2 * S + PACK * P], F32, name="late_loads", tag="late")
-        wg_a, wg_b = late_loads[:, 0:S], late_loads[:, S : 2 * S]
-        w1_second = late_loads[:, 2 * S : 2 * S + PACK * P].rearrange("p (t r) -> p t r", t=PACK)
-        nc.sync.dma_start(out=w1_second, in_=w1_rows[:, :, P : 2 * P])
-        nc.sync.dma_start(out=wg_a, in_=wg1)
+        w1_second = keep.tile([P, PACK, 256], F32, name="w1_second", tag="bg_even", align_bytes=64)
+        nc.sync.dma_start(out=w1_second[:], in_=w1_rows[:, :, 256:512])
+        wg_both = keep.tile([P, 2 * S], F32, name="wg_both", tag="tab_s", align_bytes=64)
+        wg_a, wg_b = wg_both[:, 0:S], wg_both[:, S : 2 * S]
+        for h in range(HALVES):
+            nc.sync.dma_start(out=wg_a[:, h * BANK : (h + 1) * BANK], in_=wg1[:, h * BANK : (h + 1) * BANK])
         w2_w = keep.tile([P, 2 * H], U8, name="w2_w", tag="w2_w", align_bytes=64)
         nc.sync.dma_start(out=w2_w[:].bitcast(I32), in_=w2_words[0].bitcast(I32))
-        w2_s = keep.tile([P, H], U8, name="w2_s", align_bytes=64)
-        nc.vector.memset(w2_s[:].bitcast(I32), 0)
-        load_scale_rows(nc.sync, w2_s, w2_scales[0])
         nc.sync.dma_start(out=wg_b, in_=wg2)
         v_words = []
         for h in range(HALVES):
@@ -125,59 +135,56 @@ def tile_list_peatland_ledger_features_kernel(
             per = BANK // 16
             nc.vector.tensor_copy(words[:], tab_w[:].bitcast(U32).indirect(list_tab[:, h * per : (h + 1) * per]))
             v_words.append(words)
-        quantize_w1_early(1, w1_second)
+        quantize_weights(256, group_weights([w1_second[:]], "grouped0"), "w_codes1")
 
-        w_late = keep.tile([P, PACK * (late + PASSES * N)], F32, name="w_late", tag="tab_w", align_bytes=64)
+        w_late = keep.tile([P, PACK * (512 + PASSES * N)], F32, name="w_late", tag="tab_w", align_bytes=64)
         raw_parts = []
         w0 = 0
-        for src in (w1_rows[:, :, 256:512], w1_rows[:, :, 512:H], w3[0:512, :].rearrange("(p t) n -> p t n", t=PACK), w3[512:H, :].rearrange("(p t) n -> p t n", t=PACK)):
+        for src in (w1_rows[:, :, 512:H], w3[0:512, :].rearrange("(p t) n -> p t n", t=PACK), w3[512:H, :].rearrange("(p t) n -> p t n", t=PACK)):
             width = src.shape[2]
             raw_parts.append(w_late[:, PACK * w0 : PACK * (w0 + width)].rearrange("p (t r) -> p t r", t=PACK))
             nc.sync.dma_start(out=raw_parts[-1], in_=src)
             w0 = w0 + width
 
-        def quantize_weights(first, parts, tag):
-            width = sum(part.shape[2] for part in parts)
-            grouped = keep.tile([P, width, PACK], BF16, name="w_grouped", tag=tag, align_bytes=64)
-            c0 = 0
-            for part in parts:
-                round_and_interleave(grouped[:, c0 : c0 + part.shape[2], :], part)
-                c0 = c0 + part.shape[2]
-            cols = slice(first, first + width)
-            quantize(w_codes[:, cols], w_scales[:, cols], grouped[:].rearrange("p c t -> p (c t)"))
-
-        gained, src_b, tanh_h1, bg_rows = {}, {}, {}, {}
+        gained, sinks, src_b, tanh_h1, bg_rows = {}, {}, {}, {}, {}
 
         def load_bg(c):
             bg_rows[c] = keep.tile([P, T2], F32, name="bg_rows", tag=("bg_even", "tab_w")[c % 2], align_bytes=64)
             nc.sync.dma_start(out=bg_rows[c][:], in_=bg[c * P : (c + 1) * P, :])
 
         def first_products(c):
-            gained[c] = keep.tile([P, S], F32, name="gained", tag="slot%d" % (c % 3))
-            src_b[c] = ring.tile([P, S], F32, name="src_b", bufs=3)
-            tanh_h1[c] = ring.tile([P, S], F32, name="tanh_h1", bufs=3)
+            gained[c] = keep.tile([P, S], F32, name="gained", tag="product%d" % (c % 2))
+            sinks[c] = ring.tile([P, S], F32, name="sinks")
+            tanh_h1[c] = keep.tile([P, S], F32, name="tanh_h1", tag="src_a%d" % c, align_bytes=64)
             rows = slice(c * P, (c + 1) * P)
             for h in range(HALVES):
                 cols = slice(h * BANK, (h + 1) * BANK)
                 h1 = bank(4 + h, [P, BANK], "h1")
                 nc.tensor.matmul_mx(
-                    out=h1[:], lhsT=w_codes[:, rows].bitcast(FP8X4), lhsT_scale=w_scales[:, rows],
+                    out=h1[:], lhsT=w_codes[c * P], lhsT_scale=w_scales[:, rows],
                     rhs=v_words[h][:].bitcast(FP8X4), rhs_scale=v_scales[:, cols], start=True, stop=True,
                 )
-                nc.scalar.activation(out=gained[c][:, cols], in_=h1[:], func=ACT.Copy, scale=gain_col[:, c : c + 1])
+                if c == 0:
+                    nc.vector.scalar_tensor_tensor(gained[c][:, cols], h1[:], gain_col[:, c : c + 1], wg_a[:, cols], MULT, MULT)
+                else:
+                    nc.scalar.activation(out=gained[c][:, cols], in_=h1[:], func=ACT.Copy, scale=gain_col[:, c : c + 1])
                 nc.scalar.activation(out=tanh_h1[c][:, cols], in_=h1[:], func=ACT.Tanh)
             for h in range(HALVES):
                 cols = slice(h * BANK, (h + 1) * BANK)
-                h2 = bank(h, [P, BANK], "h2")
+                h2 = bank(2 + h, [P, BANK], "h2")
                 nc.tensor.matmul_mx(
                     out=h2[:], lhsT=w2_w[:, 2 * c * P : 2 * (c + 1) * P].bitcast(FP4X4), lhsT_scale=w2_s[:, rows],
                     rhs=v_words[h][:].bitcast(FP8X4), rhs_scale=v_scales[:, cols], start=True, stop=True,
                 )
-                nc.scalar.copy(out=src_b[c][:, cols], in_=h2[:])
+                nc.scalar.copy(out=sinks[c][:, cols], in_=h2[:])
 
         def weigh(c):
-            nc.gpsimd.tensor_tensor(src_b[c][:], src_b[c][:], tanh_h1[c][:], ADD)
-            nc.gpsimd.tensor_tensor(src_b[c][:], src_b[c][:], wg_b, MULT)
+            src_b[c] = keep.tile([P, S], F32, name="src_b", tag="gate%d" % ((c - 2) % 3))
+            width = BANK if c == 0 else S
+            for c0 in range(0, S, width):
+                cols = slice(c0, c0 + width)
+                nc.gpsimd.tensor_tensor(src_b[c][:, cols], sinks[c][:, cols], tanh_h1[c][:, cols], ADD)
+                nc.gpsimd.tensor_tensor(src_b[c][:, cols], src_b[c][:, cols], wg_b[:, cols], MULT)
             if c > 0:
                 nc.gpsimd.tensor_tensor(tanh_h1[c][:], gained[c][:], wg_a, MULT)
 
@@ -186,14 +193,9 @@ def tile_list_peatland_ledger_features_kernel(
         def scatter(c):
             page_a, page_b = pages_a[c % 2], pages_b[c % 2]
             if c == 0:
-                per = BANK // 16
-                for h in range(HALVES):
-                    cols = slice(h * BANK, (h + 1) * BANK)
-                    nc.vector.tensor_tensor(
-                        page_a[:].indirect(list_a[:, h * per : (h + 1) * per]), gained[c][:, cols], wg_a[:, cols], MULT
-                    )
+                nc.vector.tensor_copy(page_a[:].indirect(list_a[:]), gained[c][:])
             nc.vector.tensor_copy(page_b[:].indirect(list_b[:]), src_b[c][:])
-            gate[c] = keep.tile([P, T2], F32, name="gate", tag="slot%d" % (c % 3))
+            gate[c] = keep.tile([P, T2], F32, name="gate", tag="product1" if c == TILES - 1 else "gate%d" % (c % 3))
             nc.scalar.activation(out=gate[c][:], in_=page_b[:], func=ACT.Sigmoid)
             if c > 0:
                 nc.vector.tensor_copy(page_a[:].indirect(list_a[:]), tanh_h1[c][:])
@@ -205,14 +207,14 @@ def tile_list_peatland_ledger_features_kernel(
             last = c == TILES - 1
             width = BANK if last else 2 * BANK
             engine = nc.vector if last else nc.gpsimd
-            gated = keep.tile([P, T2], F32, name="gated", tag="slot%d" % ((c + 1) % 3))
+            gated = keep.tile([P, T2], F32, name="gated", tag="product%d" % ((c + 1) % 2))
             for c0 in range(0, T2, width):
                 cols = slice(c0, c0 + width)
                 engine.tensor_tensor(gated[:, cols], pages_a[c % 2][:, cols], gate[c][:, cols], MULT)
             for q in range(CHUNKS):
                 if quarter == 0:
                     z_t[a, q] = keep.tile([P, BLOCKS, 2, P, 2], BF16, name="z_t%d" % q, tag="z_t%d" % q)
-                zt = bank(2 + q, [P, BLOCKS, P], "zt")
+                zt = bank(q if c == TILES - 2 and q < 2 else 2 + q, [P, BLOCKS, P], "zt")
                 for i, src in enumerate((bg_rows[c], gated)):
                     for b in range(BLOCKS):
                         m0 = q * BANK + b * P
@@ -225,7 +227,7 @@ def tile_list_peatland_ledger_features_kernel(
                     in_=zt[:].rearrange("m b (p u e) -> m b u p e", u=2, e=2),
                 )
 
-        z_codes = [keep.tile([P, T2], U32, name="z_codes%d" % a, align_bytes=64) for a in range(PASSES)]
+        z_codes = {}
         z_scales = [keep.tile([P, T2], U8, name="z_scales%d" % a, align_bytes=64) for a in range(PASSES)]
 
         def turn_back(a, q, grouped_words, engines, banks):
@@ -239,29 +241,51 @@ def tile_list_peatland_ledger_features_kernel(
                 dst = grouped_words[:, pair * BANK : (pair + 1) * BANK].rearrange("p (b m u) -> p b m u", b=2, u=2)
                 engines[pair](out=dst, in_=xt[:].rearrange("p b u m -> p b m u"))
 
-        def quantize_z(a, chunks, tag, engines, banks):
+        def group_z(a, chunks, tag, engines, banks):
             grouped = keep.tile([P, len(chunks) * BANK * PACK], BF16, name="z_grouped", tag=tag, align_bytes=64)
             for i, q in enumerate(chunks):
                 turn_back(a, q, grouped[:, i * BANK * PACK : (i + 1) * BANK * PACK].bitcast(F32), engines, banks)
+            return grouped
+
+        def quantize_z(a, chunks, grouped, codes_tag):
             cols = slice(chunks[0] * BANK, (chunks[-1] + 1) * BANK)
-            quantize(z_codes[a][:, cols], z_scales[a][:, cols], grouped[:])
+            codes = keep.tile([P, len(chunks) * BANK], U32, name="z_codes", tag=codes_tag, align_bytes=64)
+            quantize(codes[:], z_scales[a][:, cols], grouped[:])
+            for i, q in enumerate(chunks):
+                z_codes[a, q] = codes[:, i * BANK : (i + 1) * BANK].bitcast(FP8X4)
+
+        def multiply(acc, q, nt, passes):
+            cols = slice(q * BANK, (q + 1) * BANK)
+            for a in passes:
+                w0 = H + a * N + nt * P
+                nc.tensor.matmul_mx(
+                    out=acc[:], lhsT=w_codes[w0], lhsT_scale=w_scales[:, w0 : w0 + P],
+                    rhs=z_codes[a, q], rhs_scale=z_scales[a][:, cols],
+                    start=(a == passes[0]), stop=(a == passes[-1]),
+                )
+
+        partial = {}
+
+        def early_product(q, nt):
+            acc = bank(6 + len(partial) % 2, [P, BANK], "acc")
+            multiply(acc, q, nt, [0])
+            partial[q, nt] = keep.tile([P, BANK], F32, name="partial%d_%d" % (q, nt))
+            nc.scalar.copy(out=partial[q, nt][:], in_=acc[:])
 
         def last_product(q):
             cols = slice(q * BANK, (q + 1) * BANK)
             for nt in range(N_TILES):
-                acc = bank(2 + (q * N_TILES + nt) % 4, [P, BANK], "acc")
-                for a in range(PASSES):
-                    w0 = H + a * N + nt * P
-                    nc.tensor.matmul_mx(
-                        out=acc[:], lhsT=w_codes[:, w0 : w0 + P].bitcast(FP8X4), lhsT_scale=w_scales[:, w0 : w0 + P],
-                        rhs=z_codes[a][:, cols].bitcast(FP8X4), rhs_scale=z_scales[a][:, cols],
-                        start=(a == 0), stop=(a == PASSES - 1),
-                    )
+                acc = bank((0, 1, 4, 5)[(q * N_TILES + nt) % 4], [P, BANK], "acc")
                 result = ring.tile([P, BANK], F32, name="result", bufs=6)
-                if nt == 1:
-                    nc.vector.tensor_copy(out=result[:], in_=acc[:])
+                if (q, nt) in partial:
+                    multiply(acc, q, nt, [1])
+                    nc.vector.tensor_tensor(result[:], acc[:], partial[q, nt][:], ADD)
                 else:
-                    nc.scalar.copy(out=result[:], in_=acc[:])
+                    multiply(acc, q, nt, [0, 1])
+                    if nt == 1:
+                        nc.vector.tensor_copy(out=result[:], in_=acc[:])
+                    else:
+                        nc.scalar.copy(out=result[:], in_=acc[:])
                 nc.sync.dma_start(out=out[nt * P : (nt + 1) * P, cols], in_=result[:])
 
         first_products(0)
@@ -269,25 +293,30 @@ def tile_list_peatland_ledger_features_kernel(
         load_bg(0)
         first_products(1)
         weigh(1)
-        quantize_weights(256, [raw_parts[0]], "grouped0")
         first_products(2)
         for c in range(TILES):
-            if c + 1 < TILES:
-                load_bg(c + 1)
             scatter(c)
             if c == 0:
-                quantize_weights(512, [raw_parts[1][:, :, 0:256], raw_parts[1][:, :, 256:512], raw_parts[2], raw_parts[3][:, :, 0:128]], "grouped1")
-                quantize_weights(1536, [raw_parts[3][:, :, 128:N]], "grouped0")
+                grouped_wide = group_weights([raw_parts[0][:, :, 0:256], raw_parts[0][:, :, 256:512], raw_parts[1], raw_parts[2][:, :, 0:128]], "grouped1")
+                grouped_rest = group_weights([raw_parts[2][:, :, 128:N]], "grouped0")
+            if c == 1:
+                quantize_weights(512, grouped_wide, "src_a1")
+            if c == 2:
+                quantize_weights(1536, grouped_rest, "src_a2")
+            if c in (5, 6):
+                half = c - 5
+                quantize_z(0, [2 * half, 2 * half + 1], grouped_first[half], "src_a%d" % c)
+            if c + 1 < TILES:
+                load_bg(c + 1)
             combine(c)
             if c == TILES_PER_PASS - 1:
-                for half in range(2):
-                    quantize_z(0, [2 * half, 2 * half + 1], "grouped%d" % half, (nc.scalar.copy, nc.scalar.copy), (6, 7))
+                grouped_first = [group_z(0, [2 * half, 2 * half + 1], "grouped%d" % half, (nc.scalar.copy, nc.scalar.copy), (6, 7)) for half in range(2)]
             if c + 2 < TILES:
                 weigh(c + 2)
             if c + 3 < TILES:
                 first_products(c + 3)
         for q in range(CHUNKS + 1):
             if q < CHUNKS:
-                quantize_z(1, [q], "grouped%d" % (q % 2), (nc.scalar.copy, nc.vector.tensor_copy), ((6, 7), (0, 1))[q % 2])
+                quantize_z(1, [q], group_z(1, [q], "grouped%d" % (q % 2), (nc.scalar.copy, nc.vector.tensor_copy), ((6, 7), (2, 3))[q % 2]), "z_codes%d" % q)
             if q >= 1:
                 last_product(q - 1)

@@ -19,14 +19,29 @@ ACT = mybir.ActivationFunctionType
 
 P = 128
 PACK = 4
+K_PASS = P * PACK
+QUADRANT = 32
+LIST_ROWS = 16
 BANK = 512
+ALIGN = 64
 TILES = H // P
-TILES_PER_PASS = 4
+LAST = TILES - 1
+TILES_PER_PASS = K_PASS // P
 PASSES = TILES // TILES_PER_PASS
 CHUNKS = T2 // BANK
 HALVES = S // BANK
 BLOCKS = BANK // P
 N_TILES = N // P
+
+W_COLUMNS = H + PASSES * N
+W_EARLY = 2 * P
+W_WIDE = 1024
+W_REST = W_COLUMNS - 2 * W_EARLY - W_WIDE
+
+H2_BANK, H1_BANK, SUM_BANK = 2, 4, 2
+TURN_BANKS = ((6, 7), (2, 3))
+OUT_BANKS = (0, 1, 4, 5)
+RESULT_BUFS = 2 * N_TILES
 
 
 def tile_list_peatland_ledger_features_kernel(
@@ -41,23 +56,27 @@ def tile_list_peatland_ledger_features_kernel(
         def bank(b, shape, name):
             return psum.tile(shape, F32, name=name, tag="bank%d" % b)
 
-        def load_scale_rows(queue, plane, rows):
-            for q in range(4):
-                queue.dma_start(
-                    out=plane[32 * q : 32 * q + 4, :].bitcast(I32), in_=rows[4 * q : 4 * q + 4, :].bitcast(I32)
-                )
+        def tagged(shape, dtype, name, tag):
+            return keep.tile(shape, dtype, name=name, tag=tag, align_bytes=ALIGN)
 
-        def round_and_interleave(grouped, raw):
-            nc.scalar.copy(
-                out=grouped.rearrange("p (c i) t -> p c t i", i=4), in_=raw.rearrange("p t (c i) -> p c t i", i=4)
-            )
+        def load_list(name, source):
+            tile = keep.tile([P, S // LIST_ROWS], U16, name=name)
+            nc.sync.dma_start(tile[:], source)
+            return tile
+
+        def load_scale_rows(scale_tile, rows):
+            for q in range(P // QUADRANT):
+                nc.sync.dma_start(
+                    out=scale_tile[QUADRANT * q : QUADRANT * q + 4, :].bitcast(I32),
+                    in_=rows[4 * q : 4 * q + 4, :].bitcast(I32),
+                )
 
         def quantize(codes, scales, grouped):
             nc.vector.quantize_mx(out=codes.bitcast(FP8X4), scales=scales, in_=grouped)
 
-        tab_s = keep.tile([P, T], U8, name="tab_s", tag="tab_s", align_bytes=64)
+        tab_s = tagged([P, T], U8, "tab_s", "tab_s")
         nc.vector.memset(tab_s[:].bitcast(I32), 0)
-        zeros = keep.tile([P, P], F32, name="zeros", tag="tab_w", align_bytes=64)
+        zeros = tagged([P, P], F32, "zeros", "tab_w")
         nc.vector.memset(zeros[:], 0.0)
         ident = keep.tile([P, P], F32, name="ident")
         nc.gpsimd.affine_select(
@@ -65,113 +84,127 @@ def tile_list_peatland_ledger_features_kernel(
             pattern=[[-1, P]], channel_multiplier=1,
         )
 
-        list_tab = keep.tile([P, S // 16], U16, name="list_tab")
-        nc.sync.dma_start(list_tab[:], offs)
-        list_a = keep.tile([P, S // 16], U16, name="list_a")
-        nc.sync.dma_start(list_a[:], offs2)
-        list_b = keep.tile([P, S // 16], U16, name="list_b")
-        nc.sync.dma_start(list_b[:], offs3)
+        list_tab = load_list("list_tab", offs)
+        list_a = load_list("list_a", offs2)
+        list_b = load_list("list_b", offs3)
         w1_rows = w1.rearrange("(p t) r -> p t r", t=PACK)
-        w1_first = keep.tile([P, PACK, 256], F32, name="w1_first", tag="w2_w", align_bytes=64)
-        nc.sync.dma_start(out=w1_first[:], in_=w1_rows[:, :, 0:256])
-        load_scale_rows(nc.sync, tab_s, tab_scales[0])
-        tab_w = keep.tile([P, T], I32, name="tab_w", tag="tab_w", align_bytes=64)
+        w1_first = tagged([P, PACK, W_EARLY], F32, "w1_first", "w2_w")
+        nc.sync.dma_start(out=w1_first[:], in_=w1_rows[:, :, 0:W_EARLY])
+        load_scale_rows(tab_s, tab_scales[0])
+        tab_w = tagged([P, T], I32, "tab_w", "tab_w")
         nc.sync.dma_start(out=tab_w[:], in_=tab_words[0].rearrange("p t i -> p (t i)").bitcast(I32))
-        gain_rows = keep.tile([P, P], F32, name="gain_rows", tag="bg_even", align_bytes=64)
+        gain_rows = tagged([P, P], F32, "gain_rows", "bg_even")
         nc.vector.memset(gain_rows[:], 0.0)
         nc.sync.dma_start(out=gain_rows[0:TILES, :], in_=gain.rearrange("(c p) -> c p", p=P))
 
-        w2_s = keep.tile([P, H], U8, name="w2_s", align_bytes=64)
+        w2_s = tagged([P, H], U8, "w2_s", "w2_s")
         nc.vector.memset(w2_s[:].bitcast(I32), 0)
-        load_scale_rows(nc.sync, w2_s, w2_scales[0])
+        load_scale_rows(w2_s, w2_scales[0])
 
         pages_a = [keep.tile([P, T2], F32, name="page_a0")]
         pages_b = [keep.tile([P, T2], F32, name="page_b%d" % i) for i in range(2)]
-        nc.vector.memset(pages_a[0][:], 0.0)
-        nc.vector.memset(pages_b[0][:], 0.0)
-        nc.vector.memset(pages_b[1][:], 0.0)
+        for page in pages_a + pages_b:
+            nc.vector.memset(page[:], 0.0)
 
-        gain_t = bank(7, [P, P], "gain_t")
+        gain_t = bank(TURN_BANKS[0][1], [P, P], "gain_t")
         nc.tensor.transpose(gain_t[:], gain_rows[:], ident[:])
         gain_col = keep.tile([P, TILES], F32, name="gain_col")
         nc.scalar.activation(out=gain_col[:], in_=gain_t[:, 0:TILES], func=ACT.Copy)
 
-        w_scales = keep.tile([P, H + PASSES * N], U8, name="w_scales", align_bytes=64)
+        w_scales = tagged([P, W_COLUMNS], U8, "w_scales", "w_scales")
         w_codes = {}
 
-        def group_weights(parts, grouped_tag):
-            width = sum(part.shape[2] for part in parts)
-            grouped = keep.tile([P, width, PACK], BF16, name="w_grouped", tag=grouped_tag, align_bytes=64)
+        def group_weights(parts, tag):
+            grouped = tagged([P, sum(part.shape[2] for part in parts), PACK], BF16, "w_grouped", tag)
             c0 = 0
             for part in parts:
-                round_and_interleave(grouped[:, c0 : c0 + part.shape[2], :], part)
+                nc.scalar.copy(
+                    out=grouped[:, c0 : c0 + part.shape[2], :].rearrange("p (c i) t -> p c t i", i=4),
+                    in_=part.rearrange("p t (c i) -> p c t i", i=4),
+                )
                 c0 = c0 + part.shape[2]
             return grouped
 
-        def quantize_weights(first, grouped, codes_tag):
+        def quantize_weights(first, grouped, codes):
             width = grouped.shape[1]
-            codes = keep.tile([P, width], U32, name="w_codes", tag=codes_tag, align_bytes=64)
-            quantize(codes[:], w_scales[:, first : first + width], grouped[:].rearrange("p c t -> p (c t)"))
+            quantize(codes, w_scales[:, first : first + width], grouped[:].rearrange("p c t -> p (c t)"))
             for c0 in range(0, width, P):
                 w_codes[first + c0] = codes[:, c0 : c0 + P].bitcast(FP8X4)
 
-        quantize_weights(0, group_weights([w1_first[:]], "page_a1"), "w_codes0")
-        pages_a.append(keep.tile([P, T2], F32, name="page_a1", tag="page_a1", align_bytes=64))
+        first_grouped = group_weights([w1_first[:]], "page_a1")
+        quantize_weights(0, first_grouped, tagged([P, W_EARLY], U32, "codes", "w_codes0")[:])
+        pages_a.append(tagged([P, T2], F32, "page_a1", "page_a1"))
         nc.gpsimd.memset(pages_a[1][:], 0.0)
-        v_scales = keep.tile([P, S], U8, name="v_scales", align_bytes=64)
+        v_scales = tagged([P, S], U8, "v_scales", "v_scales")
         nc.vector.tensor_copy(v_scales[:], tab_s[:].indirect(list_tab[:]))
-        w1_second = keep.tile([P, PACK, 256], F32, name="w1_second", tag="bg_even", align_bytes=64)
-        nc.sync.dma_start(out=w1_second[:], in_=w1_rows[:, :, 256:512])
-        wg_both = keep.tile([P, 2 * S], F32, name="wg_both", tag="tab_s", align_bytes=64)
+
+        w1_second = tagged([P, PACK, W_EARLY], F32, "w1_second", "bg_even")
+        nc.sync.dma_start(out=w1_second[:], in_=w1_rows[:, :, W_EARLY : 2 * W_EARLY])
+        wg_both = tagged([P, 2 * S], F32, "wg_both", "tab_s")
         wg_a, wg_b = wg_both[:, 0:S], wg_both[:, S : 2 * S]
         for h in range(HALVES):
             nc.sync.dma_start(out=wg_a[:, h * BANK : (h + 1) * BANK], in_=wg1[:, h * BANK : (h + 1) * BANK])
-        w2_w = keep.tile([P, 2 * H], U8, name="w2_w", tag="w2_w", align_bytes=64)
+        w2_w = tagged([P, 2 * H], U8, "w2_w", "w2_w")
         nc.sync.dma_start(out=w2_w[:].bitcast(I32), in_=w2_words[0].bitcast(I32))
         nc.sync.dma_start(out=wg_b, in_=wg2)
+
         v_words = []
+        list_columns = BANK // LIST_ROWS
         for h in range(HALVES):
-            words = keep.tile([P, BANK], U32, name="v_words%d" % h, align_bytes=64)
-            per = BANK // 16
-            nc.vector.tensor_copy(words[:], tab_w[:].bitcast(U32).indirect(list_tab[:, h * per : (h + 1) * per]))
+            words = tagged([P, BANK], U32, "v_words", "v_words%d" % h)
+            half_list = list_tab[:, h * list_columns : (h + 1) * list_columns]
+            nc.vector.tensor_copy(words[:], tab_w[:].bitcast(U32).indirect(half_list))
             v_words.append(words)
-        quantize_weights(256, group_weights([w1_second[:]], "grouped0"), "w_codes1")
+        second_grouped = group_weights([w1_second[:]], "grouped0")
+        quantize_weights(W_EARLY, second_grouped, tagged([P, W_EARLY], U32, "codes", "w_codes1")[:])
 
-        w_late = keep.tile([P, PACK * (512 + PASSES * N)], F32, name="w_late", tag="tab_w", align_bytes=64)
-        raw_parts = []
+        w_late = tagged([P, PACK * (W_WIDE + W_REST)], F32, "w_late", "tab_w")
+        w3_rows = [w3[a * K_PASS : (a + 1) * K_PASS, :].rearrange("(p t) n -> p t n", t=PACK) for a in range(PASSES)]
+        late_parts = []
         w0 = 0
-        for src in (w1_rows[:, :, 512:H], w3[0:512, :].rearrange("(p t) n -> p t n", t=PACK), w3[512:H, :].rearrange("(p t) n -> p t n", t=PACK)):
-            width = src.shape[2]
-            raw_parts.append(w_late[:, PACK * w0 : PACK * (w0 + width)].rearrange("p (t r) -> p t r", t=PACK))
-            nc.sync.dma_start(out=raw_parts[-1], in_=src)
+        for source in [w1_rows[:, :, 2 * W_EARLY : H]] + w3_rows:
+            width = source.shape[2]
+            late_parts.append(w_late[:, PACK * w0 : PACK * (w0 + width)].rearrange("p (t r) -> p t r", t=PACK))
+            nc.sync.dma_start(out=late_parts[-1], in_=source)
             w0 = w0 + width
+        w1_late, w3_first, w3_second = late_parts
 
-        gained, sinks, src_b, tanh_h1, bg_rows = {}, {}, {}, {}, {}
+        gained, sinks, src_b, tanh_h1, bg_rows, gate, z_t = {}, {}, {}, {}, {}, {}, {}
+
+        def product_tag(c):
+            return "product%d" % (c % 2)
+
+        def gate_tag(c):
+            return "gate%d" % (c % 3)
+
+        def source_tag(c):
+            return "src_a%d" % c
 
         def load_bg(c):
-            bg_rows[c] = keep.tile([P, T2], F32, name="bg_rows", tag=("bg_even", "tab_w")[c % 2], align_bytes=64)
+            bg_rows[c] = tagged([P, T2], F32, "bg_rows", ("bg_even", "tab_w")[c % 2])
             nc.sync.dma_start(out=bg_rows[c][:], in_=bg[c * P : (c + 1) * P, :])
 
         def first_products(c):
-            gained[c] = keep.tile([P, S], F32, name="gained", tag="product%d" % (c % 2))
+            gained[c] = tagged([P, S], F32, "gained", product_tag(c))
             sinks[c] = ring.tile([P, S], F32, name="sinks")
-            tanh_h1[c] = keep.tile([P, S], F32, name="tanh_h1", tag="src_a%d" % c, align_bytes=64)
+            tanh_h1[c] = tagged([P, S], F32, "tanh_h1", source_tag(c))
             rows = slice(c * P, (c + 1) * P)
+            gain_c = gain_col[:, c : c + 1]
             for h in range(HALVES):
                 cols = slice(h * BANK, (h + 1) * BANK)
-                h1 = bank(4 + h, [P, BANK], "h1")
+                h1 = bank(H1_BANK + h, [P, BANK], "h1")
                 nc.tensor.matmul_mx(
                     out=h1[:], lhsT=w_codes[c * P], lhsT_scale=w_scales[:, rows],
                     rhs=v_words[h][:].bitcast(FP8X4), rhs_scale=v_scales[:, cols], start=True, stop=True,
                 )
                 if c == 0:
-                    nc.vector.scalar_tensor_tensor(gained[c][:, cols], h1[:], gain_col[:, c : c + 1], wg_a[:, cols], MULT, MULT)
+                    nc.vector.scalar_tensor_tensor(gained[c][:, cols], h1[:], gain_c, wg_a[:, cols], MULT, MULT)
                 else:
-                    nc.scalar.activation(out=gained[c][:, cols], in_=h1[:], func=ACT.Copy, scale=gain_col[:, c : c + 1])
+                    nc.scalar.activation(out=gained[c][:, cols], in_=h1[:], func=ACT.Copy, scale=gain_c)
                 nc.scalar.activation(out=tanh_h1[c][:, cols], in_=h1[:], func=ACT.Tanh)
             for h in range(HALVES):
                 cols = slice(h * BANK, (h + 1) * BANK)
-                h2 = bank(2 + h, [P, BANK], "h2")
+                h2 = bank(H2_BANK + h, [P, BANK], "h2")
                 nc.tensor.matmul_mx(
                     out=h2[:], lhsT=w2_w[:, 2 * c * P : 2 * (c + 1) * P].bitcast(FP4X4), lhsT_scale=w2_s[:, rows],
                     rhs=v_words[h][:].bitcast(FP8X4), rhs_scale=v_scales[:, cols], start=True, stop=True,
@@ -179,7 +212,7 @@ def tile_list_peatland_ledger_features_kernel(
                 nc.scalar.copy(out=sinks[c][:, cols], in_=h2[:])
 
         def weigh(c):
-            src_b[c] = keep.tile([P, S], F32, name="src_b", tag="gate%d" % ((c - 2) % 3))
+            src_b[c] = tagged([P, S], F32, "src_b", gate_tag(c - 2))
             width = BANK if c == 0 else S
             for c0 in range(0, S, width):
                 cols = slice(c0, c0 + width)
@@ -188,104 +221,84 @@ def tile_list_peatland_ledger_features_kernel(
             if c > 0:
                 nc.gpsimd.tensor_tensor(tanh_h1[c][:], gained[c][:], wg_a, MULT)
 
-        gate = {}
-
         def scatter(c):
             page_a, page_b = pages_a[c % 2], pages_b[c % 2]
             if c == 0:
                 nc.vector.tensor_copy(page_a[:].indirect(list_a[:]), gained[c][:])
             nc.vector.tensor_copy(page_b[:].indirect(list_b[:]), src_b[c][:])
-            gate[c] = keep.tile([P, T2], F32, name="gate", tag="product1" if c == TILES - 1 else "gate%d" % (c % 3))
+            gate[c] = tagged([P, T2], F32, "gate", product_tag(c) if c == LAST else gate_tag(c))
             nc.scalar.activation(out=gate[c][:], in_=page_b[:], func=ACT.Sigmoid)
             if c > 0:
                 nc.vector.tensor_copy(page_a[:].indirect(list_a[:]), tanh_h1[c][:])
 
-        z_t = {}
-
         def combine(c):
             a, quarter = divmod(c, TILES_PER_PASS)
-            last = c == TILES - 1
-            width = BANK if last else 2 * BANK
-            engine = nc.vector if last else nc.gpsimd
-            gated = keep.tile([P, T2], F32, name="gated", tag="product%d" % ((c + 1) % 2))
+            engine, width = (nc.vector, BANK) if c == LAST else (nc.gpsimd, 2 * BANK)
+            gated = tagged([P, T2], F32, "gated", product_tag(c + 1))
             for c0 in range(0, T2, width):
                 cols = slice(c0, c0 + width)
                 engine.tensor_tensor(gated[:, cols], pages_a[c % 2][:, cols], gate[c][:, cols], MULT)
             for q in range(CHUNKS):
                 if quarter == 0:
                     z_t[a, q] = keep.tile([P, BLOCKS, 2, P, 2], BF16, name="z_t%d" % q, tag="z_t%d" % q)
-                zt = bank(q if c == TILES - 2 and q < 2 else 2 + q, [P, BLOCKS, P], "zt")
-                for i, src in enumerate((bg_rows[c], gated)):
+                sum_bank = OUT_BANKS[q - 2] if c == LAST - 1 and q >= 2 else SUM_BANK + q
+                zt = bank(sum_bank, [P, BLOCKS, P], "zt")
+                for i, term in enumerate((bg_rows[c], gated)):
                     for b in range(BLOCKS):
                         m0 = q * BANK + b * P
                         nc.tensor.matmul(
-                            zt[:, b, :], lhsT=src[:, m0 : m0 + P], rhs=ident[:], is_transpose=True,
+                            zt[:, b, :], lhsT=term[:, m0 : m0 + P], rhs=ident[:], is_transpose=True,
                             start=(i == 0 and b == 0), stop=(i == 1 and b == BLOCKS - 1),
                         )
                 nc.scalar.copy(
-                    out=z_t[a, q][:, :, :, 32 * quarter : 32 * (quarter + 1), :],
+                    out=z_t[a, q][:, :, :, QUADRANT * quarter : QUADRANT * (quarter + 1), :],
                     in_=zt[:].rearrange("m b (p u e) -> m b u p e", u=2, e=2),
                 )
 
         z_codes = {}
-        z_scales = [keep.tile([P, T2], U8, name="z_scales%d" % a, align_bytes=64) for a in range(PASSES)]
+        z_scales = [tagged([P, T2], U8, "z_scales", "z_scales%d" % a) for a in range(PASSES)]
 
-        def turn_back(a, q, grouped_words, engines, banks):
-            words = z_t[a, q][:].rearrange("m b u p e -> m (b u p e)").bitcast(F32)
-            for pair in range(2):
-                xt = bank(banks[pair], [P, 2, 2, P], "xt")
-                for b in range(2):
-                    for u in range(2):
-                        w0 = ((2 * pair + b) * 2 + u) * P
-                        nc.tensor.transpose(xt[:, b, u, :], words[:, w0 : w0 + P], ident[:])
-                dst = grouped_words[:, pair * BANK : (pair + 1) * BANK].rearrange("p (b m u) -> p b m u", b=2, u=2)
-                engines[pair](out=dst, in_=xt[:].rearrange("p b u m -> p b m u"))
-
-        def group_z(a, chunks, tag, engines, banks):
-            grouped = keep.tile([P, len(chunks) * BANK * PACK], BF16, name="z_grouped", tag=tag, align_bytes=64)
+        def group_z(a, chunks, tag, copies, banks):
+            grouped = tagged([P, len(chunks) * BANK * PACK], BF16, "z_grouped", tag)
             for i, q in enumerate(chunks):
-                turn_back(a, q, grouped[:, i * BANK * PACK : (i + 1) * BANK * PACK].bitcast(F32), engines, banks)
+                grouped_words = grouped[:, i * BANK * PACK : (i + 1) * BANK * PACK].bitcast(F32)
+                words = z_t[a, q][:].rearrange("m b u p e -> m (b u p e)").bitcast(F32)
+                for pair in range(2):
+                    xt = bank(banks[pair], [P, 2, 2, P], "xt")
+                    for b in range(2):
+                        for u in range(2):
+                            x0 = ((2 * pair + b) * 2 + u) * P
+                            nc.tensor.transpose(xt[:, b, u, :], words[:, x0 : x0 + P], ident[:])
+                    copies[pair](
+                        out=grouped_words[:, pair * BANK : (pair + 1) * BANK].rearrange("p (b m u) -> p b m u", b=2, u=2),
+                        in_=xt[:].rearrange("p b u m -> p b m u"),
+                    )
             return grouped
 
-        def quantize_z(a, chunks, grouped, codes_tag):
-            cols = slice(chunks[0] * BANK, (chunks[-1] + 1) * BANK)
-            codes = keep.tile([P, len(chunks) * BANK], U32, name="z_codes", tag=codes_tag, align_bytes=64)
-            quantize(codes[:], z_scales[a][:, cols], grouped[:])
-            for i, q in enumerate(chunks):
-                z_codes[a, q] = codes[:, i * BANK : (i + 1) * BANK].bitcast(FP8X4)
+        def quantize_z(a, q, grouped, codes):
+            quantize(codes, z_scales[a][:, q * BANK : (q + 1) * BANK], grouped)
+            z_codes[a, q] = codes.bitcast(FP8X4)
 
-        def multiply(acc, q, nt, passes):
-            cols = slice(q * BANK, (q + 1) * BANK)
-            for a in passes:
-                w0 = H + a * N + nt * P
-                nc.tensor.matmul_mx(
-                    out=acc[:], lhsT=w_codes[w0], lhsT_scale=w_scales[:, w0 : w0 + P],
-                    rhs=z_codes[a, q], rhs_scale=z_scales[a][:, cols],
-                    start=(a == passes[0]), stop=(a == passes[-1]),
-                )
-
-        partial = {}
-
-        def early_product(q, nt):
-            acc = bank(6 + len(partial) % 2, [P, BANK], "acc")
-            multiply(acc, q, nt, [0])
-            partial[q, nt] = keep.tile([P, BANK], F32, name="partial%d_%d" % (q, nt))
-            nc.scalar.copy(out=partial[q, nt][:], in_=acc[:])
+        def quantize_first_pass(q, codes):
+            c0 = (q % 2) * BANK * PACK
+            quantize_z(0, q, first_pass[q // 2][:, c0 : c0 + BANK * PACK], codes)
 
         def last_product(q):
             cols = slice(q * BANK, (q + 1) * BANK)
             for nt in range(N_TILES):
-                acc = bank((0, 1, 4, 5)[(q * N_TILES + nt) % 4], [P, BANK], "acc")
-                result = ring.tile([P, BANK], F32, name="result", bufs=6)
-                if (q, nt) in partial:
-                    multiply(acc, q, nt, [1])
-                    nc.vector.tensor_tensor(result[:], acc[:], partial[q, nt][:], ADD)
+                acc = bank(OUT_BANKS[(q * N_TILES + nt) % len(OUT_BANKS)], [P, BANK], "acc")
+                result = ring.tile([P, BANK], F32, name="result", bufs=RESULT_BUFS)
+                for a in range(PASSES):
+                    n0 = H + a * N + nt * P
+                    nc.tensor.matmul_mx(
+                        out=acc[:], lhsT=w_codes[n0], lhsT_scale=w_scales[:, n0 : n0 + P],
+                        rhs=z_codes[a, q], rhs_scale=z_scales[a][:, cols],
+                        start=(a == 0), stop=(a == PASSES - 1),
+                    )
+                if nt == 1:
+                    nc.vector.tensor_copy(out=result[:], in_=acc[:])
                 else:
-                    multiply(acc, q, nt, [0, 1])
-                    if nt == 1:
-                        nc.vector.tensor_copy(out=result[:], in_=acc[:])
-                    else:
-                        nc.scalar.copy(out=result[:], in_=acc[:])
+                    nc.scalar.copy(out=result[:], in_=acc[:])
                 nc.sync.dma_start(out=out[nt * P : (nt + 1) * P, cols], in_=result[:])
 
         first_products(0)
@@ -294,29 +307,38 @@ def tile_list_peatland_ledger_features_kernel(
         first_products(1)
         weigh(1)
         first_products(2)
+        in_wide = N - W_REST
         for c in range(TILES):
             scatter(c)
             if c == 0:
-                grouped_wide = group_weights([raw_parts[0][:, :, 0:256], raw_parts[0][:, :, 256:512], raw_parts[1], raw_parts[2][:, :, 0:128]], "grouped1")
-                grouped_rest = group_weights([raw_parts[2][:, :, 128:N]], "grouped0")
+                wide_parts = [w1_late[:, :, 0:W_EARLY], w1_late[:, :, W_EARLY : 2 * W_EARLY], w3_first, w3_second[:, :, 0:in_wide]]
+                wide_grouped = group_weights(wide_parts, "grouped1")
+                rest_grouped = group_weights([w3_second[:, :, in_wide:N]], "w3_grouped")
             if c == 1:
-                quantize_weights(512, grouped_wide, "src_a1")
-            if c == 2:
-                quantize_weights(1536, grouped_rest, "src_a2")
-            if c in (5, 6):
-                half = c - 5
-                quantize_z(0, [2 * half, 2 * half + 1], grouped_first[half], "src_a%d" % c)
-            if c + 1 < TILES:
+                quantize_weights(2 * W_EARLY, wide_grouped, tagged([P, W_WIDE], U32, "codes", source_tag(c))[:])
+            if c == LAST:
+                quantize_first_pass(0, tagged([P, BANK], U32, "codes", source_tag(c))[:])
+            if c < LAST:
                 load_bg(c + 1)
             combine(c)
             if c == TILES_PER_PASS - 1:
-                grouped_first = [group_z(0, [2 * half, 2 * half + 1], "grouped%d" % half, (nc.scalar.copy, nc.scalar.copy), (6, 7)) for half in range(2)]
+                first_pass = [
+                    group_z(0, [2 * i, 2 * i + 1], "grouped%d" % i, (nc.scalar.copy, nc.scalar.copy), TURN_BANKS[0])
+                    for i in range(2)
+                ]
             if c + 2 < TILES:
                 weigh(c + 2)
             if c + 3 < TILES:
                 first_products(c + 3)
+
+        held = tagged([P, (CHUNKS - 1) * BANK + W_REST], U32, "codes", product_tag(LAST))
+        for q in range(1, CHUNKS):
+            quantize_first_pass(q, held[:, (q - 1) * BANK : q * BANK])
+        quantize_weights(W_COLUMNS - W_REST, rest_grouped, held[:, (CHUNKS - 1) * BANK : (CHUNKS - 1) * BANK + W_REST])
         for q in range(CHUNKS + 1):
             if q < CHUNKS:
-                quantize_z(1, [q], group_z(1, [q], "grouped%d" % (q % 2), (nc.scalar.copy, nc.vector.tensor_copy), ((6, 7), (2, 3))[q % 2]), "z_codes%d" % q)
+                copies = (nc.scalar.copy, nc.vector.tensor_copy)
+                second_pass = group_z(1, [q], "last_grouped%d" % (q % 2), copies, TURN_BANKS[q % 2])
+                quantize_z(1, q, second_pass[:], tagged([P, BANK], U32, "codes", "z_codes%d" % q)[:])
             if q >= 1:
                 last_product(q - 1)

from contextlib import ExitStack

import concourse.mybir as mybir

K, T, S, T2, H, N = 512, 4096, 1024, 2048, 1024, 384
FLOPS = 2 * K * H * S * 2 + 2 * H * N * T2

F32 = mybir.dt.float32
BF16 = mybir.dt.bfloat16
I32 = mybir.dt.int32
U32 = mybir.dt.uint32
U16 = mybir.dt.uint16
U8 = mybir.dt.uint8
FP8X4 = mybir.dt.float8_e4m3fn_x4
FP4X4 = mybir.dt.float4_e2m1fn_x4
MULT = mybir.AluOpType.mult
ADD = mybir.AluOpType.add
ACT = mybir.ActivationFunctionType

P = 128
PACK = 4
K_PASS = P * PACK
QUADRANT = 32
LIST_ROWS = 16
BANK = 512
ALIGN = 64
TILES = H // P
LAST = TILES - 1
TILES_PER_PASS = K_PASS // P
PASSES = TILES // TILES_PER_PASS
CHUNKS = T2 // BANK
HALVES = S // BANK
BLOCKS = BANK // P
N_TILES = N // P

W_COLUMNS = H + PASSES * N
W_EARLY = 2 * P
W_WIDE = 1024
W_REST = W_COLUMNS - 2 * W_EARLY - W_WIDE

H2_BANK, H1_BANK, SUM_BANK = 2, 4, 2
TURN_BANKS = ((6, 7), (2, 3))
OUT_BANKS = (0, 1, 4, 5)
RESULT_BUFS = 2 * N_TILES


def tile_list_peatland_ledger_features_kernel(
    tc, tab_words, tab_scales, offs, offs2, offs3, w1, w2_words, w2_scales, w3, gain, bg, wg1, wg2, out
):
    nc = tc.nc
    with ExitStack() as ctx:
        keep = ctx.enter_context(tc.tile_pool(name="keep", bufs=1))
        ring = ctx.enter_context(tc.tile_pool(name="ring", bufs=2))
        psum = ctx.enter_context(tc.psum_pool(name="psum", bufs=1))

        def bank(b, shape, name):
            return psum.tile(shape, F32, name=name, tag="bank%d" % b)

        def tagged(shape, dtype, name, tag):
            return keep.tile(shape, dtype, name=name, tag=tag, align_bytes=ALIGN)

        def load_list(name, source):
            tile = keep.tile([P, S // LIST_ROWS], U16, name=name)
            nc.sync.dma_start(tile[:], source)
            return tile

        def load_scale_rows(scale_tile, rows):
            for q in range(P // QUADRANT):
                nc.sync.dma_start(
                    out=scale_tile[QUADRANT * q : QUADRANT * q + 4, :].bitcast(I32),
                    in_=rows[4 * q : 4 * q + 4, :].bitcast(I32),
                )

        def quantize(codes, scales, grouped):
            nc.vector.quantize_mx(out=codes.bitcast(FP8X4), scales=scales, in_=grouped)

        tab_s = tagged([P, T], U8, "tab_s", "tab_s")
        nc.vector.memset(tab_s[:].bitcast(I32), 0)
        zeros = tagged([P, P], F32, "zeros", "tab_w")
        nc.vector.memset(zeros[:], 0.0)
        ident = keep.tile([P, P], F32, name="ident")
        nc.gpsimd.affine_select(
            out=ident[:], in_=zeros[:], compare_op=mybir.AluOpType.not_equal, fill=1.0, base=0,
            pattern=[[-1, P]], channel_multiplier=1,
        )

        list_tab = load_list("list_tab", offs)
        list_a = load_list("list_a", offs2)
        list_b = load_list("list_b", offs3)
        w1_rows = w1.rearrange("(p t) r -> p t r", t=PACK)
        w1_first = tagged([P, PACK, W_EARLY], F32, "w1_first", "w2_w")
        nc.sync.dma_start(out=w1_first[:], in_=w1_rows[:, :, 0:W_EARLY])
        load_scale_rows(tab_s, tab_scales[0])
        tab_w = tagged([P, T], I32, "tab_w", "tab_w")
        nc.sync.dma_start(out=tab_w[:], in_=tab_words[0].rearrange("p t i -> p (t i)").bitcast(I32))
        gain_rows = tagged([P, P], F32, "gain_rows", "bg_even")
        nc.vector.memset(gain_rows[:], 0.0)
        nc.sync.dma_start(out=gain_rows[0:TILES, :], in_=gain.rearrange("(c p) -> c p", p=P))

        w2_s = tagged([P, H], U8, "w2_s", "w2_s")
        nc.vector.memset(w2_s[:].bitcast(I32), 0)
        load_scale_rows(w2_s, w2_scales[0])

        pages_a = [keep.tile([P, T2], F32, name="page_a0")]
        pages_b = [keep.tile([P, T2], F32, name="page_b%d" % i) for i in range(2)]
        for page in pages_a + pages_b:
            nc.vector.memset(page[:], 0.0)

        gain_t = bank(TURN_BANKS[0][1], [P, P], "gain_t")
        nc.tensor.transpose(gain_t[:], gain_rows[:], ident[:])
        gain_col = keep.tile([P, TILES], F32, name="gain_col")
        nc.scalar.activation(out=gain_col[:], in_=gain_t[:, 0:TILES], func=ACT.Copy)

        w_scales = tagged([P, W_COLUMNS], U8, "w_scales", "w_scales")
        w_codes = {}

        def group_weights(parts, tag):
            grouped = tagged([P, sum(part.shape[2] for part in parts), PACK], BF16, "w_grouped", tag)
            c0 = 0
            for part in parts:
                nc.scalar.copy(
                    out=grouped[:, c0 : c0 + part.shape[2], :].rearrange("p (c i) t -> p c t i", i=4),
                    in_=part.rearrange("p t (c i) -> p c t i", i=4),
                )
                c0 = c0 + part.shape[2]
            return grouped

        def quantize_weights(first, grouped, codes):
            width = grouped.shape[1]
            quantize(codes, w_scales[:, first : first + width], grouped[:].rearrange("p c t -> p (c t)"))
            for c0 in range(0, width, P):
                w_codes[first + c0] = codes[:, c0 : c0 + P].bitcast(FP8X4)

        first_grouped = group_weights([w1_first[:]], "page_a1")
        quantize_weights(0, first_grouped, tagged([P, W_EARLY], U32, "codes", "w_codes0")[:])
        pages_a.append(tagged([P, T2], F32, "page_a1", "page_a1"))
        nc.gpsimd.memset(pages_a[1][:], 0.0)
        v_scales = tagged([P, S], U8, "v_scales", "v_scales")
        nc.vector.tensor_copy(v_scales[:], tab_s[:].indirect(list_tab[:]))

        w1_second = tagged([P, PACK, W_EARLY], F32, "w1_second", "bg_even")
        nc.sync.dma_start(out=w1_second[:], in_=w1_rows[:, :, W_EARLY : 2 * W_EARLY])
        wg_both = tagged([P, 2 * S], F32, "wg_both", "tab_s")
        wg_a, wg_b = wg_both[:, 0:S], wg_both[:, S : 2 * S]
        for h in range(HALVES):
            nc.sync.dma_start(out=wg_a[:, h * BANK : (h + 1) * BANK], in_=wg1[:, h * BANK : (h + 1) * BANK])
        w2_w = tagged([P, 2 * H], U8, "w2_w", "w2_w")
        nc.sync.dma_start(out=w2_w[:].bitcast(I32), in_=w2_words[0].bitcast(I32))
        nc.sync.dma_start(out=wg_b, in_=wg2)

        v_words = []
        list_columns = BANK // LIST_ROWS
        for h in range(HALVES):
            words = tagged([P, BANK], U32, "v_words", "v_words%d" % h)
            half_list = list_tab[:, h * list_columns : (h + 1) * list_columns]
            nc.vector.tensor_copy(words[:], tab_w[:].bitcast(U32).indirect(half_list))
            v_words.append(words)
        second_grouped = group_weights([w1_second[:]], "grouped0")
        quantize_weights(W_EARLY, second_grouped, tagged([P, W_EARLY], U32, "codes", "w_codes1")[:])

        w_late = tagged([P, PACK * (W_WIDE + W_REST)], F32, "w_late", "tab_w")
        w3_rows = [w3[a * K_PASS : (a + 1) * K_PASS, :].rearrange("(p t) n -> p t n", t=PACK) for a in range(PASSES)]
        late_parts = []
        w0 = 0
        for source in [w1_rows[:, :, 2 * W_EARLY : H]] + w3_rows:
            width = source.shape[2]
            late_parts.append(w_late[:, PACK * w0 : PACK * (w0 + width)].rearrange("p (t r) -> p t r", t=PACK))
            nc.sync.dma_start(out=late_parts[-1], in_=source)
            w0 = w0 + width
        w1_late, w3_first, w3_second = late_parts

        gained, sinks, src_b, tanh_h1, bg_rows, gate, z_t = {}, {}, {}, {}, {}, {}, {}

        def product_tag(c):
            return "product%d" % (c % 2)

        def gate_tag(c):
            return "gate%d" % (c % 3)

        def source_tag(c):
            return "src_a%d" % c

        def load_bg(c):
            bg_rows[c] = tagged([P, T2], F32, "bg_rows", ("bg_even", "tab_w")[c % 2])
            nc.sync.dma_start(out=bg_rows[c][:], in_=bg[c * P : (c + 1) * P, :])

        def first_products(c):
            gained[c] = tagged([P, S], F32, "gained", product_tag(c))
            sinks[c] = ring.tile([P, S], F32, name="sinks")
            tanh_h1[c] = tagged([P, S], F32, "tanh_h1", source_tag(c))
            rows = slice(c * P, (c + 1) * P)
            gain_c = gain_col[:, c : c + 1]
            for h in range(HALVES):
                cols = slice(h * BANK, (h + 1) * BANK)
                h1 = bank(H1_BANK + h, [P, BANK], "h1")
                nc.tensor.matmul_mx(
                    out=h1[:], lhsT=w_codes[c * P], lhsT_scale=w_scales[:, rows],
                    rhs=v_words[h][:].bitcast(FP8X4), rhs_scale=v_scales[:, cols], start=True, stop=True,
                )
                if c == 0:
                    nc.vector.scalar_tensor_tensor(gained[c][:, cols], h1[:], gain_c, wg_a[:, cols], MULT, MULT)
                else:
                    nc.scalar.activation(out=gained[c][:, cols], in_=h1[:], func=ACT.Copy, scale=gain_c)
                nc.scalar.activation(out=tanh_h1[c][:, cols], in_=h1[:], func=ACT.Tanh)
            for h in range(HALVES):
                cols = slice(h * BANK, (h + 1) * BANK)
                h2 = bank(H2_BANK + h, [P, BANK], "h2")
                nc.tensor.matmul_mx(
                    out=h2[:], lhsT=w2_w[:, 2 * c * P : 2 * (c + 1) * P].bitcast(FP4X4), lhsT_scale=w2_s[:, rows],
                    rhs=v_words[h][:].bitcast(FP8X4), rhs_scale=v_scales[:, cols], start=True, stop=True,
                )
                nc.scalar.copy(out=sinks[c][:, cols], in_=h2[:])

        def weigh(c):
            src_b[c] = tagged([P, S], F32, "src_b", gate_tag(c - 2))
            width = BANK if c == 0 else S
            for c0 in range(0, S, width):
                cols = slice(c0, c0 + width)
                nc.gpsimd.tensor_tensor(src_b[c][:, cols], sinks[c][:, cols], tanh_h1[c][:, cols], ADD)
                nc.gpsimd.tensor_tensor(src_b[c][:, cols], src_b[c][:, cols], wg_b[:, cols], MULT)
            if c > 0:
                nc.gpsimd.tensor_tensor(tanh_h1[c][:], gained[c][:], wg_a, MULT)

        def scatter(c):
            page_a, page_b = pages_a[c % 2], pages_b[c % 2]
            if c == 0:
                nc.vector.tensor_copy(page_a[:].indirect(list_a[:]), gained[c][:])
            nc.vector.tensor_copy(page_b[:].indirect(list_b[:]), src_b[c][:])
            gate[c] = tagged([P, T2], F32, "gate", product_tag(c) if c == LAST else gate_tag(c))
            nc.scalar.activation(out=gate[c][:], in_=page_b[:], func=ACT.Sigmoid)
            if c > 0:
                nc.vector.tensor_copy(page_a[:].indirect(list_a[:]), tanh_h1[c][:])

        def combine(c):
            a, quarter = divmod(c, TILES_PER_PASS)
            engine, width = (nc.vector, BANK) if c == LAST else (nc.gpsimd, 2 * BANK)
            gated = tagged([P, T2], F32, "gated", product_tag(c + 1))
            for c0 in range(0, T2, width):
                cols = slice(c0, c0 + width)
                engine.tensor_tensor(gated[:, cols], pages_a[c % 2][:, cols], gate[c][:, cols], MULT)
            for q in range(CHUNKS):
                if quarter == 0:
                    z_t[a, q] = keep.tile([P, BLOCKS, 2, P, 2], BF16, name="z_t%d" % q, tag="z_t%d" % q)
                sum_bank = OUT_BANKS[q - 2] if c == LAST - 1 and q >= 2 else SUM_BANK + q
                zt = bank(sum_bank, [P, BLOCKS, P], "zt")
                for i, term in enumerate((bg_rows[c], gated)):
                    for b in range(BLOCKS):
                        m0 = q * BANK + b * P
                        nc.tensor.matmul(
                            zt[:, b, :], lhsT=term[:, m0 : m0 + P], rhs=ident[:], is_transpose=True,
                            start=(i == 0 and b == 0), stop=(i == 1 and b == BLOCKS - 1),
                        )
                nc.scalar.copy(
                    out=z_t[a, q][:, :, :, QUADRANT * quarter : QUADRANT * (quarter + 1), :],
                    in_=zt[:].rearrange("m b (p u e) -> m b u p e", u=2, e=2),
                )

        z_codes = {}
        z_scales = [tagged([P, T2], U8, "z_scales", "z_scales%d" % a) for a in range(PASSES)]

        def group_z(a, chunks, tag, copies, banks):
            grouped = tagged([P, len(chunks) * BANK * PACK], BF16, "z_grouped", tag)
            for i, q in enumerate(chunks):
                grouped_words = grouped[:, i * BANK * PACK : (i + 1) * BANK * PACK].bitcast(F32)
                words = z_t[a, q][:].rearrange("m b u p e -> m (b u p e)").bitcast(F32)
                for pair in range(2):
                    xt = bank(banks[pair], [P, 2, 2, P], "xt")
                    for b in range(2):
                        for u in range(2):
                            x0 = ((2 * pair + b) * 2 + u) * P
                            nc.tensor.transpose(xt[:, b, u, :], words[:, x0 : x0 + P], ident[:])
                    copies[pair](
                        out=grouped_words[:, pair * BANK : (pair + 1) * BANK].rearrange("p (b m u) -> p b m u", b=2, u=2),
                        in_=xt[:].rearrange("p b u m -> p b m u"),
                    )
            return grouped

        def quantize_z(a, q, grouped, codes):
            quantize(codes, z_scales[a][:, q * BANK : (q + 1) * BANK], grouped)
            z_codes[a, q] = codes.bitcast(FP8X4)

        def quantize_first_pass(q, codes):
            c0 = (q % 2) * BANK * PACK
            quantize_z(0, q, first_pass[q // 2][:, c0 : c0 + BANK * PACK], codes)

        def last_product(q):
            cols = slice(q * BANK, (q + 1) * BANK)
            for nt in range(N_TILES):
                acc = bank(OUT_BANKS[(q * N_TILES + nt) % len(OUT_BANKS)], [P, BANK], "acc")
                result = ring.tile([P, BANK], F32, name="result", bufs=RESULT_BUFS)
                for a in range(PASSES):
                    n0 = H + a * N + nt * P
                    nc.tensor.matmul_mx(
                        out=acc[:], lhsT=w_codes[n0], lhsT_scale=w_scales[:, n0 : n0 + P],
                        rhs=z_codes[a, q], rhs_scale=z_scales[a][:, cols],
                        start=(a == 0), stop=(a == PASSES - 1),
                    )
                if nt == 1:
                    nc.vector.tensor_copy(out=result[:], in_=acc[:])
                else:
                    nc.scalar.copy(out=result[:], in_=acc[:])
                nc.sync.dma_start(out=out[nt * P : (nt + 1) * P, cols], in_=result[:])

        first_products(0)
        weigh(0)
        load_bg(0)
        first_products(1)
        weigh(1)
        first_products(2)
        in_wide = N - W_REST
        for c in range(TILES):
            scatter(c)
            if c == 0:
                wide_parts = [w1_late[:, :, 0:W_EARLY], w1_late[:, :, W_EARLY : 2 * W_EARLY], w3_first, w3_second[:, :, 0:in_wide]]
                wide_grouped = group_weights(wide_parts, "grouped1")
                rest_grouped = group_weights([w3_second[:, :, in_wide:N]], "w3_grouped")
            if c == 1:
                quantize_weights(2 * W_EARLY, wide_grouped, tagged([P, W_WIDE], U32, "codes", source_tag(c))[:])
            if c == LAST:
                quantize_first_pass(0, tagged([P, BANK], U32, "codes", source_tag(c))[:])
            if c < LAST:
                load_bg(c + 1)
            combine(c)
            if c == TILES_PER_PASS - 1:
                first_pass = [
                    group_z(0, [2 * i, 2 * i + 1], "grouped%d" % i, (nc.scalar.copy, nc.scalar.copy), TURN_BANKS[0])
                    for i in range(2)
                ]
            if c + 2 < TILES:
                weigh(c + 2)
            if c + 3 < TILES:
                first_products(c + 3)

        held = tagged([P, (CHUNKS - 1) * BANK + W_REST], U32, "codes", product_tag(LAST))
        for q in range(1, CHUNKS):
            quantize_first_pass(q, held[:, (q - 1) * BANK : q * BANK])
        quantize_weights(W_COLUMNS - W_REST, rest_grouped, held[:, (CHUNKS - 1) * BANK : (CHUNKS - 1) * BANK + W_REST])
        for q in range(CHUNKS + 1):
            if q < CHUNKS:
                copies = (nc.scalar.copy, nc.vector.tensor_copy)
                second_pass = group_z(1, [q], "last_grouped%d" % (q % 2), copies, TURN_BANKS[q % 2])
                quantize_z(1, q, second_pass[:], tagged([P, BANK], U32, "codes", "z_codes%d" % q)[:])
            if q >= 1:
                last_product(q - 1)
